import numpy as np, ml_dtypes
CORES = [113,118,241,246]
N = 4
BF = ml_dtypes.bfloat16
def f(rng, *shape):
    return (rng.standard_normal(shape, dtype=np.float32) * np.exp2(rng.integers(-2, 3, shape[:-1] + (1,)))).astype(BF)
def wide(rng, *shape):
    v = f(rng, *shape).astype(np.float32); k = shape[:-2] + (1, shape[-1])
    return (v * np.exp2(rng.integers(-6, 7, k)) * (rng.random(k) > 0.0625)).astype(BF)
def gentries(a):
    return np.ascontiguousarray(a.reshape(8, 16, -1).transpose(0, 2, 1)).reshape(8, -1)
def gtable(e):
    e = np.asarray(e); return np.ascontiguousarray(e.reshape(8, -1, 16).transpose(0, 2, 1)).reshape(128, -1).astype(np.int32)
R, S, P, CAPP, SM = 4096, 64, 16, 768, 512
D, W = 2 * S * P, 512 // P
ST = np.arange(D) // (2 * P)
def draws(a, b, cn):
    u = ((a * np.arange(D) + b) >> 2) & 1023
    m = (u * np.sum(cn, 0)[:, ST]) >> 10
    return m, np.sum(m >= np.add.accumulate(cn, 0)[:, :, ST], 0)
def most(own):
    return np.max(np.stack([np.sum(own == q, 1) for q in range(N)]), 0)
def parts(rng, tot, k, hi):
    v = []
    for i in range(k - 1, -1, -1):
        e = int(rng.integers(max(1, tot - i * hi), min(hi, tot - i) + 1)); v.append(e); tot -= e
    return rng.permutation(v)
def latin(rng, al, small):
    cn = np.zeros((N, 8, S), np.int64); turn = (np.arange(N)[:, None] + np.arange(N)) % N
    for g in range(8):
        t = np.concatenate([[1, SM], parts(rng, R - 1 - SM, S // N - 2, SM)]) if small else parts(rng, R, S // N, SM)
        cn[:, g] = np.concatenate([rng.multinomial(e, rng.dirichlet(np.full(N, al)))[turn] for e in t], 1)[:, rng.permutation(S)]
    return cn
def sole(rng):
    cn = np.zeros((N, 8, S), np.int64); q = rng.integers(0, N); k = CAPP // (2 * P)
    for g in range(8):
        n = [k] + [(S - k + i) // (N - 1) for i in range(N - 1)]; o = rng.permutation(np.repeat((q + g + np.arange(N)) % N, n))
        for i in range(N):
            p = np.flatnonzero(o == i); cn[i, g, p] = parts(rng, R, len(p), SM)
    return cn
def even(rng, ends):
    low = rng.choice([0, W - 1], (8, 1)) if ends else rng.integers(0, W, (8, 1))
    return 4 * W * (2 * rng.integers(0, P, (8, 1)) + 1), 4 * (W * rng.integers(0, 2 * P, (8, 1)) + low) + rng.integers(0, 4, (8, 1))
def keys(rng, cn):
    out = []
    for r in range(N):
        a, b = even(rng, False)
        for t in range(4):
            c, e = rng.integers(256, 3841, (8, 1)), rng.integers(0, 4096, (8, 1)); ok = (most(draws(c, e, cn)[1]) <= CAPP)[:, None]
            a, b = np.where(ok, c, a), np.where(ok, e, b)
        out += [a, b]
    return np.concatenate(out, 1)
def make(rng, cn, ab):
    return {"x": f(rng, N, 128, R), "idx": np.stack([gtable(rng.permuted(np.tile(np.arange(R), (8, 1)), axis=1)) for r in range(N)]),
            "counts": cn.astype(np.int32), "ab": np.tile(ab[None], (N, 1, 1)).astype(np.int32)}
def setup_inputs(rng):
    cn = latin(rng, 2.0, False); return make(rng, cn, keys(rng, cn))
def setup_inputs_full(rng):
    ab = rng.integers(0, 4096, (8, 2 * N)); g = rng.integers(0, 8, N); k = 2 * np.arange(N)
    ab[g, k] = 0; ab[(g + 1) % 8, k] = rng.integers(1, 16, N); ab[(g + 2) % 8, k] = 4095; ab[(g + 3) % 8, k] = rng.integers(1024, 3072, N)
    return make(rng, sole(rng), ab)
def setup_inputs_ends(rng):
    d = make(rng, latin(rng, 1.0, False), np.concatenate([e for r in range(N) for e in even(rng, True)], 1))
    d["idx"] = np.stack([gtable(np.where(rng.random((8, 1)) < 0.5, np.arange(R), np.arange(R)[::-1])) for r in range(N)]); return d
def setup_inputs_uneven(rng):
    cn = latin(rng, 0.2, True); return make(rng, cn, keys(rng, cn))
def setup_inputs_spread(rng):
    d = setup_inputs(rng); d["x"] = wide(rng, N, 128, R); return d
def check_inputs(d):
    bad = []; cn = d["counts"].astype(np.int64); ab = d["ab"].astype(np.int64); sz = np.sum(cn, 0)
    if not np.isfinite(d["x"].astype(np.float32)).all(): bad.append("finite")
    if not all((np.sort(gentries(i), 1) == np.arange(R)).all() for i in d["idx"]): bad.append("each_row_once")
    if cn.min() < 0 or (np.sum(cn, 2) != R).any(): bad.append("counts")
    if sz.min() < 1 or sz.max() > SM: bad.append("sizes")
    if ab.min() < 0 or ab.max() > 4095 or (ab != ab[:1]).any(): bad.append("constants")
    if not bad and any(most(draws(ab[0][:, 2 * r:2 * r + 1], ab[0][:, 2 * r + 1:2 * r + 2], cn)[1]).max() > CAPP for r in range(N)): bad.append("cap")
    return bad
def reference(x, idx, counts, ab):
    cn = counts.astype(np.int64); start = np.add.accumulate(cn, 2) - cn; before = np.add.accumulate(cn, 0) - cn
    rows = np.stack([gentries(i) for i in idx]).astype(np.int64); X = x.astype(np.float32).reshape(N, 8, 16, R)
    G = np.arange(8)[:, None]; y = np.zeros((N, 128, S), np.float32)
    for r in range(N):
        c = ab[r].astype(np.int64); m, own = draws(c[:, 2 * r:2 * r + 1], c[:, 2 * r + 1:2 * r + 2], cn)
        row = rows[own, G, start[own, G, ST] + m - before[own, G, ST]]
        v = X[own, G, :, row].reshape(8, S, P, 2, 16)
        z = np.abs(v[:, :, :, 0] - v[:, :, :, 1]); h = P
        while h > 1:
            h >>= 1; z = z[:, :, :h] + z[:, :, h:]
        y[r] = z[:, :, 0].transpose(0, 2, 1).reshape(128, S)
    return {"y": y}

@@ -1,0 +1,492 @@
+from concourse.bass import DstId, RemoteDMATransfer
+from concourse.mybir import AluOpType, ActivationFunctionType
+
+F32, I32, U16, BF, F16 = "float32", "int32", "uint16", "bfloat16", "float16"
+R, CAP = 4096, 768
+TAG = 16384
+WIN = 240
+
+_SB = {
+    BF: dict(xin=R, big=R + 3 * CAP, outb=3 * CAP, bo16=128, ub16=128, zm=144, rst=512, sgn=64, hr=96, ltl=384, lth=384,
+             pl=384, ph=384, cnt=56, lto=384, pr=384, nr=56, gw=1024),
+    I32: dict(idxi=256, cl=16, abz=8, pci=4, j2i=24, tb=(32, 16), ui=512, wli=4, wla=4, yp=128, npos=128, ci=144, li=96,
+              dd=96, et=384, eu=384, win=3 * WIN, wm=144, eni=128),
+    U16: dict(idxu=256, bcl=32, j2=24, pml=8, yl=4, l16=96, ls=96, lst=144, fl=128),
+    F16: dict(uf=384),
+    F32: dict(abf=8, abv=8, colf=4, cst=8, xf=144, i16=128, g16=128, pm8=8, oc0=48, oc=48, kc=48, bo32=128, u32=128, msk=128,
+              mtab=32, i2=32, nb=128, n0r=128, tagc=8, k3c=8, lf=2, cf=4, inc=4, one4=4, e1=4, st=4, st2=4, stc=8, us=384,
+              ufo=128, uso=128, key=8, wsc=4, kex=64, rk2=4, wtab=48, crep=384, wv=4, f1=32, f2=32, cg=128, bb=16, xw=16,
+              xe=256, offm=4, zn=24, nf=48, hh=48, dst=96, ep=384, em=384, ee=384, ea=384, eb=408, es=384, tsx=48, kt=32,
+              kk=32, dk=24, yo=128, en=128, epo=128, own=128, acc=640, ac2=256, ac3=128, ac4=128, df=1024, zs=512, tr=640,
+              ys=64),
+}
+SCRATCH = {n: ("sbuf", [128] + (list(s) if isinstance(s, tuple) else [s]), d) for d, t in _SB.items() for n, s in t.items()}
+SCRATCH.update({n: ("psum", [128, 512], F32) for n in ("psab", "psk", "psh", "psrep", "pst", "psr", "psz0", "psz1")})
+SEMAPHORES = ["sv", "sa", "st", "sg", "ldc", "lda", "ldi", "ldx", "go", "carr", "csent", "darr", "dsent", "sty"]
+
+A = AluOpType
+AF = ActivationFunctionType
+
+
+def _bits(engs):
+    m = 0
+    for e in engs:
+        m |= 1 << e
+    return m
+
+
+def _peers(rank, T, topo):
+    c = T.cores[rank]
+    others = [q for q in range(len(T.cores)) if q != rank]
+    near = [q for q in others if T.cores[q] in topo.cores_of(c)]
+    return [q for q in others if q not in near] + near
+
+
+def _count_engines(rank, T, topo):
+    c = T.cores[rank]
+    used, out = [], []
+    for q in _peers(rank, T, topo):
+        e = [k for k in topo.engines(c, T.cores[q]) if k not in used][:4]
+        used += e
+        out.append(e)
+    return out
+
+
+def _data_engines(rank, T, topo):
+    c = T.cores[rank]
+    peers = _peers(rank, T, topo)
+    far = set()
+    for q in peers:
+        if T.cores[q] not in topo.cores_of(c):
+            far |= set(topo.engines(c, T.cores[q]))
+    out = []
+    for q in peers:
+        e = topo.engines(c, T.cores[q])
+        if T.cores[q] in topo.cores_of(c):
+            e = [k for k in e if k not in far] or e
+        out.append(e)
+    return out
+
+
+def _arrange(ops):
+    lastw, readers = {}, {}
+    for n, o in enumerate(ops):
+        d = set()
+        for k in o["r"] + o["w"]:
+            if k in lastw:
+                d.add(lastw[k])
+        for k in o["w"]:
+            d |= set(readers.get(k, []))
+        o["d"] = d
+        for k in o["r"]:
+            readers.setdefault(k, []).append(n)
+        for k in o["w"]:
+            lastw[k] = n
+            readers[k] = []
+    level = [0.0] * len(ops)
+    for n in range(len(ops) - 1, -1, -1):
+        level[n] += ops[n]["c"] + ops[n]["lat"]
+        for d in ops[n]["d"]:
+            level[d] = max(level[d], level[n])
+    end, free, out, left = {}, {}, [], list(range(len(ops)))
+    while left:
+        can = []
+        for n in left:
+            if all(d in end for d in ops[n]["d"]):
+                can.append((max([free.get(ops[n]["q"], 0.0)] + [end[d] for d in ops[n]["d"]]), n))
+        t0, n0 = min(can)
+        n = max((level[m], -m) for t, m in can if ops[m]["q"] == ops[n0]["q"] and t <= t0 + 0.05)[1]
+        n = -n
+        t = [t for t, m in can if m == n][0]
+        if ops[n]["q"] != "x":
+            free[ops[n]["q"]] = t + ops[n]["c"]
+        end[n] = t + ops[n]["c"] + ops[n]["lat"]
+        left.remove(n)
+        out.append(ops[n])
+    return out
+
+
+def rank_program(g, core, T, topo):
+    me = T.rank_of(core)
+    if me is None:
+        return
+    peers = _peers(me, T, topo)
+    slots = peers + [me]
+    V, S, PE, SY = g.vector, g.scalar, g.tensor, g.sync
+    ops = []
+
+    def rec(q, make, r, w, c, lat=0.16, ev=None):
+        ops.append(dict(q=q, make=make, r=r.split(), w=w.split(), c=c, lat=lat, ev=ev))
+
+    def cyc(n):
+        return 0.04 + 0.00104 * max(64, n)
+
+    def mm(items, r, w, n, group=True):
+        def make():
+            for k, (o, l, rh) in enumerate(items):
+                ins = PE.matmul(o, l, rh, (k == 0) or not group, (k == len(items) - 1) or not group)
+            return ins
+        rec("t", make, r, w, cyc(n))
+
+    def ts1(out, in0, s1, op0, r, w, n=64):
+        rec("v", lambda: V.tensor_scalar(out, in0, s1, None, op0), r, w, cyc(n))
+
+    def ts2(out, in0, s1, s2, op0, op1, r, w, n=64):
+        rec("v", lambda: V.tensor_scalar(out, in0, s1, s2, op0, op1), r, w, cyc(n))
+
+    def tt(out, in0, in1, o, r, w, n=64):
+        rec("v", lambda: V.tensor_tensor(out, in0, in1, o), r, w, cyc(n))
+
+    def cp(out, in_, r, w, n=64):
+        rec("v", lambda: V.tensor_copy(out, in_), r, w, cyc(n))
+
+    def scan(out, d0, d1, o0, o1, r, w, n=64):
+        rec("v", lambda: V.tensor_tensor_scan(out, d0, d1, 0.0, o0, o1), r, w, cyc(n))
+
+    def act(out, in_, r, w, n=64, func=AF.Identity, **kw):
+        rec("a", lambda: S.activation(out, in_, func, **kw), r, w, cyc(n))
+
+    def iota(out, pattern, base, cm, w, n, r="go", whole=False):
+        kw = {} if whole else dict(allow_small_or_imprecise_dtypes=True)
+        rec("g", lambda: g.iota(out, pattern, base, cm, **kw), r, w, 0.13 + 0.0021 * n)
+
+    def fill(out, n, val, w, whole=False):
+        iota(out, [[0, n]], val, 0, w, n, whole=whole)
+
+    def load(q, out, in_, sem, val, r, w, lat):
+        rec(q, lambda: (SY if q == "s" else S).dma_start(out, in_).then_inc(T.sem[sem], 16), r, w, 0.05, lat, (sem, val))
+
+    def suffix(ps, n, r, w):
+        mm([(ps[:, 0:48], T.ub16[:], n[:, 0:48])] + [(ps[:, 0:48], T.bo16[:], n[:, d:d + 48]) for d in range(1, 8)],
+           "ub16 bo16 " + r, w, 512)
+
+    SHR, AND, MUL, ADD, SUB = A.arith_shift_right, A.bitwise_and, A.mult, A.add, A.subtract
+    cengs, dengs = _count_engines(me, T, topo), _data_engines(me, T, topo)
+    carr = sum(len(_count_engines(q, T, topo)[_peers(q, T, topo).index(me)]) for q in peers)
+    darr = sum(len(_data_engines(q, T, topo)[_peers(q, T, topo).index(me)]) for q in peers)
+    mine = T.cl[:, 4 * me:4 * me + 4]
+
+    load("s", mine, T.counts[:], "ldc", 16, "", "clme q1", 2.0)
+    rec("v", lambda: V.memset(T.abz[:], 0), "", "abz", 0.1)
+    load("s", T.abz[0:128:16, :], T.ab[:], "lda", 16, "", "abz", 2.0)
+    load("a", T.idxi[:], T.idx[:], "ldi", 16, "", "idxi", 2.2)
+    rec("x", None, "", "q2", 0.0, 0.4)
+    load("s", T.xin[:, 0:R // 2], T.x[:, 0:R // 2], "ldx", 16, "q2", "xa", 3.5)
+
+    def send_counts():
+        trs = []
+        for q, e in zip(peers, cengs):
+            rid, pid = topo.addr(T.cores[q], core)
+            trs.append(RemoteDMATransfer(dst_ids=[DstId(rid=rid, pnc=pid)], dma_engine_mask=_bits(e), remote_sem=T.sem.carr,
+                                         src=mine, dst=mine))
+        g.remote_dma_fused(trs, local_sem=T.sem.csent)
+        g.sem_inc(T.sem.go, 1)
+
+    rec("g", send_counts, "clme", "go", 0.3, 0.1, ("go", 1))
+    rec("x", None, "go", "clfar", 0.0, 3.5, ("carr", carr))
+    load("s", T.xin[:, R // 2:R], T.x[:, R // 2:R], "ldx", 32, "go", "xin", 3.5)
+
+    iota(T.pci[:, 0:1], [[0, 1]], 0, 1, "p", 1, "", True)
+    iota(T.g16[:], [[1, 8], [0, 16]], 0, 0, "g16", 128, "")
+    iota(T.xf[:], [[1, 144]], 0, 0, "xf", 144, "")
+    iota(T.i16[:], [[0, 8], [1, 16]], 0, 0, "i16", 128, "")
+    iota(T.n0r[:], [[16, 8], [128, 16]], 0, 0, "n0r", 128)
+    iota(T.oc0[:], [[0, 3], [16, 16]], 0, 0, "oc0", 48)
+    iota(T.pm8[:], [[1, 2], [16, 2], [8, 2]], 0, 0, "pm8", 8)
+    iota(T.i2[:], [[0, 2], [2, 16]], -15, 0, "i2", 32)
+    iota(T.j2i[:], [[1, 12], [0, 2]], 0, 0, "j2i", 24, whole=True)
+    rec("g", lambda: g.affine_select(T.u32[:], T.bo32[:], [[-1, 128]], A.is_ge, 0.0, 0, 1), "go bo32", "u32", 0.44)
+    fill(T.cnt[:], 56, 0, "cnt0")
+    fill(T.nr[:], 56, 0, "nr0")
+    fill(T.xw[:], 16, 0, "xw0")
+    fill(T.ci[:, 96:144], 48, 0, "rho0", True)
+    fill(T.kk[:, 8 * me:8 * me + 8], 8, 0, "kk%d" % me)
+    for k in range(3):
+        fill(T.eb[:, 136 * k:136 * k + 1], 1, 0, "eb0%d" % k)
+        fill(T.win[:, WIN * k:WIN * k + 48], 48, 0, "w%d" % k, True)
+    rec("v", lambda: V.memset(T.rst[:], 1.0), "", "rst", cyc(256))
+    rec("v", lambda: V.memset(T.rst[:, 0:512:16], 0.0), "", "rst", cyc(64))
+    rec("v", lambda: V.memset(T.one4[:], 1.0), "", "one4", cyc(64))
+    lane, grp = T.colf[:, 1:2], T.colf[:, 2:3]
+    ts1(T.pci[:, 1:2], T.pci[:, 0:1], 15, AND, "p", "lanei")
+    ts1(T.pci[:, 2:3], T.pci[:, 0:1], 4, SHR, "p", "grpi")
+    ts1(T.pci[:, 3:4], T.pci[:, 1:2], 2, SHR, "lanei", "l2")
+    cp(T.colf[:, 0:3], T.pci[:, 0:3], "p lanei grpi", "colf")
+    act(T.cst[:, 0:1], lane, "colf", "lane128", scale=128.0)
+    act(T.cst[:, 1:2], grp, "colf", "c15", scale=16.0, bias=15.0)
+    act(T.cst[:, 2:3], lane, "colf", "lanetag", scale=float(TAG), bias=float(4096 + 2 ** 23))
+    act(T.cst[:, 4:5], lane, "colf", "lane4", scale=4.0)
+    act(T.cst[:, 5:6], lane, "colf", "lane32", scale=32.0)
+    act(T.nb[:], T.xf[:, 0:128], "xf lane128", "nb", 128, bias=T.cst[:, 0:1])
+    act(T.tagc[:], T.xf[:, 0:8], "xf lanetag", "tagc", scale=float(16 * TAG), bias=T.cst[:, 2:3])
+    act(T.oc[:], T.oc0[:], "oc0 colf", "oc", bias=lane)
+    act(T.kc[:], T.oc[:], "oc", "kc", bias=64.0)
+    act(T.bo16[:], T.bo32[:], "bo32", "bo16", 128)
+    act(T.ub16[:], T.u32[:], "u32", "ub16", 128)
+    ts1(T.bo32[:], T.g16[:], grp, A.is_equal, "g16 colf", "bo32", 128)
+    ops.insert(0, ops.pop())
+    ts1(T.msk[:], T.i16[:], lane, A.is_equal, "i16 colf", "msk", 128)
+    cp(T.bcl[:], T.xf[:, 0:32], "xf", "bcl")
+    ts1(T.zm[:], T.xf[:], T.cst[:, 1:2], A.is_equal, "xf c15", "zm", 144)
+    ts1(T.mtab[:], T.xf[:, 0:32], lane, A.is_le, "xf colf", "mtab")
+    cp(T.j2[:], T.j2i[:], "j2i", "j2")
+    ts2(T.lf[:, 0:1], T.pci[:, 3:4], -126.0, T.cst[:, 5:6], MUL, ADD, "l2 lane32", "lf0")
+    ts1(T.yl[:], T.xf[:, 0:4], T.cst[:, 4:5], ADD, "xf lane4", "yl")
+    ts1(T.pml[:], T.pm8[:], T.lf[:, 0:1], ADD, "pm8 lf0", "pml")
+    base = {q: float(R + CAP * peers.index(q) + CAP + 15) for q in peers}
+    if me != 3:
+        act(T.lf[:, 1:2], lane, "colf", "lf1", scale=16.0, bias=base[3] - 2048.0)
+        act(T.k3c[:], T.xf[:, 0:8], "xf lf1", "k3c", scale=256.0, bias=T.lf[:, 1:2])
+    made = {k: o for o in ops for k in o["w"]}
+    head = []
+
+    def first(o):
+        if not any(o is h for h in head):
+            for k in o["r"]:
+                first(made[k])
+            head.append(o)
+
+    for o in list(ops):
+        first(o)
+    ops[:] = head
+
+    cp(T.abf[:], T.abz[:], "abz", "abf")
+    mm([(T.psab[:, 0:8], T.bo32[:], T.abf[:])], "bo32 abf", "psab", 256)
+    cp(T.abv[:], T.psab[:, 0:8], "psab", "abv")
+    cp(T.cf[:], mine, "clme", "cf")
+    scan(T.inc[:], T.one4[:], T.cf[:], MUL, ADD, "one4 cf", "inc")
+    mm([(T.psr[:, 0:4], T.u32[:], T.inc[:])], "u32 inc", "psr", 256)
+    tt(T.e1[:], T.inc[:], T.cf[:], SUB, "inc cf", "e1")
+    ts2(T.st[:], T.e1[:], T.psr[:, 3:4], float(R), SUB, ADD, "e1 psr", "st")
+    tt(T.stc[:, 0:8:2], T.tagc[:, 0:8:2], T.st[:], ADD, "tagc st", "stc0")
+    tt(T.stc[:, 1:8:2], T.tagc[:, 1:8:2], T.st[:], ADD, "tagc st", "stc1")
+
+    def ac(q):
+        return T.abv[:, 2 * q:2 * q + 1]
+
+    def bc(q):
+        return T.abv[:, 2 * q + 1:2 * q + 2]
+
+    for k in range(3):
+        ts2(T.tb[:, k:24:3, :], T.nb[:], ac(slots[k]), bc(slots[k]), MUL, ADD, "nb abv", "tb%d" % k, 128)
+        act(T.crep[:, 128 * k:128 * k + 128], T.n0r[:], "n0r abv", "crep%d" % k, 128, scale=ac(slots[k]), bias=bc(slots[k]))
+    ts2(T.tb[:, 24:32, :], T.nb[:], ac(me), bc(me), MUL, ADD, "nb abv", "tb3", 128)
+    ts2(T.ui[:, 0:384], T.tb[:, 0:24, :], 2, 1023, SHR, AND, "tb0 tb1 tb2", "ui", 384)
+    ts2(T.ui[:, 384:512], T.tb[:, 24:32, :], 2, 1023, SHR, AND, "tb3", "uio", 128)
+    ts1(T.uf[:], T.ui[:, 0:384], 1.0 / 1024, MUL, "ui", "uf", 384)
+    ts1(T.ufo[:], T.ui[:, 384:512], 1.0 / 1024, MUL, "uio", "ufo", 128)
+    ts1(T.wli[:], T.abv[:, 0:8:2], lane, MUL, "abv colf", "wli")
+    ts1(T.wla[:], T.wli[:], 4095, AND, "wli", "wla")
+    ts2(T.key[:, 0:4], T.wla[:], 16.0, lane, MUL, ADD, "wla colf", "key")
+    ts2(T.wsc[:], T.wla[:], 1.0 / 4096, -1.0, MUL, ADD, "wla", "wsc")
+    tt(T.kex[:], T.key[:, 0:4].indirect(T.bcl[:, 0:4]), T.msk[:, 0:64], MUL, "key bcl msk", "kex", 120)
+    mm([(T.psk[:, 0:64], T.bo32[:], T.kex[:]), (T.psk[:, 64:68], T.bo32[:], T.wsc[:])], "bo32 kex wsc", "psk", 512, False)
+    for q in slots:
+        act(T.sgn[:, 16 * q:16 * q + 16], T.psk[:, 16 * q:16 * q + 16], "psk key", "sgn%d rk%d" % (q, q),
+            func=AF.Sign, scale=-1.0, bias=T.key[:, q:q + 1], accum_out=T.rk2[:, q:q + 1])
+    act(T.wv[:], T.psk[:, 64:68], "psk", "wv", scale=-1.0, bias=0.25)
+    for k in range(3):
+        ts2(T.hr[:, k:96:3], T.i2[:], T.rk2[:, slots[k]:slots[k] + 1], lane, A.is_equal, MUL, "i2 colf rk%d" % slots[k],
+            "hr%d" % k)
+    mm([(T.psh[:, 0:48], T.zm[:, 15 - k:143 - k], T.hr[:, 3 * k:3 * k + 48]) for k in range(16)], "zm hr0 hr1 hr2", "psh", 1024)
+    for k in range(3):
+        ts1(T.wtab[:, 16 * k:16 * k + 16], T.psh[:, k:48:3], ac(slots[k]), MUL, "psh abv", "wtab%d" % k)
+    mm([(T.psab[:, 16 * k:16 * k + 16], T.bo16[:], T.sgn[:, 16 * me:16 * me + 16]) for k in range(8)],
+       "bo16 sgn%d" % me, "psab", 512, False)
+    scan(T.us[:], T.rst[:, 0:384], T.uf[:], MUL, ADD, "rst uf", "us", 384)
+    scan(T.uso[:], T.rst[:, 0:128], T.ufo[:], MUL, ADD, "rst ufo", "uso", 128)
+    for k in range(3):
+        ts2(T.f1[:, k:24:3], T.uf[:, 16 * k:384:48], -16.0, T.wv[:, slots[k]:slots[k] + 1], MUL, ADD, "uf wv", "f1%d" % k)
+    tt(T.f2[:, 0:24], T.us[:, 15:384:16], T.f1[:, 0:24], ADD, "us f10 f11 f12", "z")
+    ts2(T.f1[:, 24:32], T.ufo[:, 0:128:16], -16.0, T.wv[:, me:me + 1], MUL, ADD, "ufo wv", "f13")
+    tt(T.f2[:, 24:32], T.uso[:, 15:128:16], T.f1[:, 24:32], ADD, "uso f13", "zo")
+
+    cp(T.idxu[:], T.idxi[:], "idxi", "idxu", 256)
+    late = "crep0 crep1 crep2 wv oc kc ub16 " + " ".join("rk%d" % q for q in slots)
+    act(T.big[:, 0:R], T.xin[:].indirect(T.idxu[:]), "xin idxu " + late, "xs", 6400, func=AF.Copy)
+
+    cq = [T.cl[:, 4 * q:4 * q + 4] for q in range(4)]
+    bnd = {1: T.bb[:, 0:4], 2: T.bb[:, 4:8], 3: T.bb[:, 8:12]}
+    tt(bnd[2], cq[0], cq[1], ADD, "clme clfar", "b2")
+    tt(T.bb[:, 12:16], cq[2], cq[3], ADD, "clme clfar", "b23")
+    cp(bnd[1], cq[0], "clme clfar", "b1")
+    tt(T.xw[:, 0:4], bnd[2], T.bb[:, 12:16], ADD, "xw0 b2 b23", "size")
+    tt(bnd[3], bnd[2], cq[2], ADD, "b2 clme clfar", "b3")
+    lo, hi = me, me + 1
+
+    def under(out, nout, b, key):
+        for j in range(4):
+            ts2(out[:, 96 * j:96 * j + 96], T.uf[:, 96 * j:96 * j + 96], T.xw[:, j:j + 1], bnd[b][:, j:j + 1], MUL, A.is_lt,
+                "uf size b%d" % b, "%s%d" % (key, j))
+        scan(nout[:], T.rst[:, 0:384], out[:], MUL, ADD, "rst #0 #1 #2 #3".replace("#", key), "n" + key, 192)
+
+    for hh in range(2):
+        o, s = T.xw[:, 8 + hh:16:2], T.stc[:, hh:8:2]
+        if me == 0:
+            cp(o, s, "xw0 stc%d" % hh, "off%d" % hh)
+        else:
+            tt(o, s, bnd[lo], SUB, "xw0 stc%d b%d" % (hh, lo), "off%d" % hh)
+    if me != 0:
+        under(T.ltl, T.pl, lo, "lo")
+    if me != 3:
+        under(T.lth, T.ph, hi, "hi")
+    for k in range(3):
+        o, e = T.cnt[:, 16 * k:16 * k + 8], slice(16 * k + 15, 384, 48)
+        if me == 0:
+            cp(o, T.ph[:, e], "cnt0 nhi", "cnt%d" % (k + 1))
+        elif me == 3:
+            ts2(o, T.pl[:, e], -1.0, 16.0, MUL, ADD, "cnt0 nlo", "cnt%d" % (k + 1))
+        else:
+            tt(o, T.ph[:, e], T.pl[:, e], SUB, "cnt0 nlo nhi", "cnt%d" % (k + 1))
+    suffix(T.pst, T.cnt, "cnt1 cnt2 cnt3", "pst")
+    tt(T.xe[:, 0:128], T.xw[:].indirect(T.j2[:, 0:8]), T.msk[:], MUL, "size off0 off1 j2 msk", "xe0", 220)
+    tt(T.xe[:, 128:256], T.xw[:].indirect(T.bcl[:, 8:16]), T.msk[:], MUL, "size off0 off1 bcl msk", "xe1", 220)
+    mm([(T.psrep[:, 0:256], T.bo32[:], T.xe[:])], "bo32 xe0 xe1", "psrep", 1024)
+
+    ts2(T.ci[:, 48:96], T.pst[:, 0:48], -1.0, float(CAP), MUL, ADD, "pst", "ci")
+    if me == 0:
+        zn = T.f2
+    else:
+        zn = T.zn
+        tt(T.zn[:], T.pl[:, 15:384:16], T.f2[:, 0:24], ADD, "nlo z", "zn")
+    tt(T.ci[:, 0:48], T.ci[:, 48:96], T.cnt[:, 0:48], ADD, "ci cnt1 cnt2 cnt3", "ce", 96)
+    for k in range(3):
+        tt(T.ci[:, 96 + 16 * k:104 + 16 * k], zn[:, k:24:3], T.pst[:, 16 * k:16 * k + 8], ADD, "rho0 z zn pst", "rho%d" % (k + 1))
+    ts1(T.li[:], T.ci[:, 48:144], 15, AND, "ci rho1 rho2 rho3", "li", 96)
+    cp(T.l16[:], T.li[:], "li", "l16", 96)
+    ts1(T.dd[:], T.ci[:, 0:96], 4, SHR, "ci ce", "dd", 96)
+    tt(T.nf[:], T.dd[:, 0:48], T.dd[:, 48:96], A.is_equal, "dd", "nf", 96)
+    tt(T.hh[:], T.nf[:], T.kc[:], MUL, "nf kc", "hh", 96)
+    tt(T.dst[:, 0:48], T.hh[:], T.dd[:, 48:96], ADD, "hh dd", "dst", 96)
+    tt(T.dst[:, 48:96], T.oc[:], T.hh[:], SUB, "hh oc", "lbf", 96)
+    cp(T.ls[:], T.dst[:], "dst lbf", "ls", 96)
+
+    def chain(k):
+        c = slice(128 * k, 128 * k + 128)
+        u = slice(16 * k, 16 * k + 8)
+        u2 = slice(48 + 16 * k, 56 + 16 * k)
+        m = slice(48 * k, 48 * k + 48)
+        e0, w0, q = 136 * k, WIN * k, peers[k]
+
+        def n(s):
+            return s.replace("#", str(k))
+        tt(T.et[:, c], T.wtab[:, 16 * k:16 * k + 16].indirect(T.l16[:, u2]), T.crep[:, c], ADD, n("wtab# l16 crep#"), n("et#"), 220)
+        ts2(T.eu[:, c], T.et[:, c], 2, 1023, SHR, AND, n("et#"), n("eu#"), 128)
+        tt(T.ep[:, c], T.eu[:, c], T.psrep[:, 0:128], MUL, n("eu# psrep"), n("ep#"), 128)
+        act(T.em[:, c], T.ep[:, c], n("ep#"), n("em#"), 128, scale=1.0 / 1024, bias=-0.5 + 2.0 ** -11)
+        tt(T.ee[:, c], T.em[:, c], T.psrep[:, 128:256], ADD, n("em# psrep"), n("ee#"), 128)
+        tt(T.ea[:, c], T.mtab[:].indirect(T.l16[:, u]), T.ee[:, c], MUL, n("mtab l16 ee#"), n("ea#"), 220)
+        act(T.eb[:, e0 + 1:e0 + 129], T.ee[:, c].indirect(T.ls[:, u2]), n("ls ee#"), n("ebb#"), 220, func=AF.Copy)
+        scan(T.es[:, c], T.eb[:, e0:e0 + 128], T.ea[:, c], A.max, A.max, n("eb0# ebb# ea#"), n("es#"), 128)
+        cp(T.win[:, w0:w0 + WIN].indirect(T.ls[:, u]), T.es[:, c], n("ls es#"), n("w#"), 490)
+        ts1(T.wm[:, m], T.win[:, w0:w0 + 48], R - 1, AND, n("w#"), n("wm#"))
+        cp(T.lst[:, m], T.wm[:, m], n("wm#"), n("lst#"))
+        src = T.outb[:, CAP * k:CAP * k + CAP]
+        act(src, T.big[:, 0:R].indirect(T.lst[:, m]), n("xs lst#"), n("out#"), 1220, func=AF.Copy)
+        rid, pid = topo.addr(T.cores[q], core)
+        at = R + CAP * _peers(q, T, topo).index(me)
+        rec("g", lambda: g.remote_dma(T.big[:, at:at + CAP], src, T.sem.darr, T.sem.dsent, pid, rid, _bits(dengs[k])),
+            n("out#") + (" sent0" if k == 1 else ""), n("sent#"), 0.3, (2.0, 4.5, 3.5)[k], ("", 0))
+
+    for k in range(3):
+        chain(k)
+    rec("x", None, "sent0 sent1 sent2", "land", 0.0, 0.0, ("darr", darr))
+
+    act(T.cg[:], T.psab[:, 0:128], "psab xs", "cg", 128, scale=0.5, bias=7.5)
+    ts1(T.st2[:], T.st[:], -0.5 + 2.0 ** -11, ADD, "st", "st2")
+    if me == 0:
+        offm, offk = T.st2, "st2"
+    else:
+        tt(T.offm[:], T.st2[:], bnd[lo], SUB, "st2 b%d" % lo, "offm")
+        offm, offk = T.offm, "offm"
+    for j in range(4):
+        c = slice(32 * j, 32 * j + 32)
+        act(T.yo[:, c], T.ufo[:, c], "ufo size xs", "yo%d" % j, scale=T.xw[:, j:j + 1])
+        act(T.en[:, c], T.ufo[:, c], "ufo size xs " + offk, "en%d" % j, scale=T.xw[:, j:j + 1], bias=offm[:, j:j + 1])
+
+    def lto(b):
+        return T.lto[:, 128 * b - 128:128 * b]
+
+    for b in (1, 2, 3):
+        tt(lto(b), T.bb[:].indirect(T.j2[:, 8 * b - 8:8 * b]), T.yo[:], A.is_gt, "b1 b2 b3 b23 j2 yo0 yo1 yo2 yo3", "lt%d" % b, 220)
+    scan(T.pr[:], T.rst[:, 0:384], T.lto[:], MUL, ADD, "rst lt1 lt2 lt3", "pr", 192)
+    for b in (1, 2, 3):
+        cp(T.nr[:, 16 * b - 16:16 * b - 8], T.pr[:, 128 * b - 113:128 * b:16], "nr0 pr", "nr%d" % b)
+    suffix(T.psr, T.nr, "nr1 nr2 nr3", "psr")
+    tt(T.yp[:], T.f2[:, 24:32].indirect(T.bcl[:, 0:8]), T.cg[:], ADD, "zo bcl cg", "yp", 220)
+    ts1(T.npos[:], T.yp[:], 15, AND, "yp", "npos", 128)
+    cp(T.eni[:], T.en[:], "en0 en1 en2 en3", "eni", 128)
+    tt(T.tsx[:], T.psr[:, 0:48], T.nr[:, 0:48], SUB, "psr nr1 nr2 nr3", "tsx")
+    if me != 0:
+        ts2(T.kk[:, 0:8], T.psr[:, 0:8], -1.0, base[0], MUL, ADD, "psr", "kk0")
+    tt(T.epo[:], T.eni[:], T.npos[:], ADD, "eni npos", "epo", 256)
+    for q in (1, 2):
+        if q != me:
+            tt(T.kt[:, 8 * q:8 * q + 8], T.tsx[:, 16 * q - 16:16 * q - 8], T.psr[:, 16 * q:16 * q + 8], SUB, "tsx psr", "kt%d" % q)
+            ts1(T.kk[:, 8 * q:8 * q + 8], T.kt[:, 8 * q:8 * q + 8], base[q], ADD, "kt%d" % q, "kk%d" % q)
+    if me != 3:
+        tt(T.kk[:, 24:32], T.tsx[:, 32:40], T.k3c[:], ADD, "tsx k3c", "kk3")
+    if me == 0:
+        tt(T.psz0[:, 0:128], T.epo[:], lto(1), MUL, "epo lt1", "psz0", 256)
+    else:
+        if me == 3:
+            act(T.own[:], lto(3), "lt3", "own", 128, scale=-1.0, bias=1.0)
+        else:
+            tt(T.own[:], lto(hi), lto(lo), SUB, "lt%d lt%d" % (hi, lo), "own", 256)
+        tt(T.psz0[:, 0:128], T.epo[:], T.own[:], MUL, "epo own", "psz0", 256)
+    tt(T.dk[:], T.kk[:, 0:24], T.kk[:, 8:32], SUB, "kk0 kk1 kk2 kk3", "dk")
+    tt(T.acc[:, 0:128], T.kk[:, 24:32].indirect(T.bcl[:, 0:8]), T.npos[:], SUB, "kk3 bcl npos", "acc0", 220)
+    tt(T.acc[:, 128:512], T.dk[:].indirect(T.bcl[:, 0:24]), T.lto[:], MUL, "dk bcl lt1 lt2 lt3", "acc1", 620)
+    tt(T.psz0[:, 0:128], T.psz0[:, 0:128], T.acc[:, 0:128], ADD, "acc0", "psz0", 128)
+    tt(T.ac2[:, 0:128], T.acc[:, 128:256], T.acc[:, 256:384], ADD, "acc1", "ac2a", 256)
+    tt(T.psz0[:, 0:128], T.psz0[:, 0:128], T.acc[:, 384:512], ADD, "acc1", "psz0", 128)
+    tt(T.ac4[:], T.psz0[:, 0:128], T.ac2[:, 0:128], ADD, "ac2a psz0", "ac4", 128)
+    cp(T.fl[:], T.ac4[:].indirect(T.pml[:]), "ac4 pml", "fl", 220)
+
+    zout = [T.psz0[:, 0:256], T.zs[:, 0:256], T.psz1[:, 0:256], T.zs[:, 256:512]]
+    for k, (f, key) in enumerate(zip((0, 32, 16, 48), ("psz0", "zs1", "psz1", "zs3"))):
+        c = slice(256 * k, 256 * k + 256)
+        act(T.gw[:, c], T.big[:].indirect(T.fl[:, 64 + f:80 + f]), "xs land fl", "gw%d" % k, 420, func=AF.Copy)
+        tt(T.df[:, c], T.big[:].indirect(T.fl[:, f:f + 16]), T.gw[:, c], SUB, "xs land fl gw%d" % k, "df%d" % k, 420)
+        act(zout[k], T.df[:, c], "df%d" % k, key, 256, func=AF.Abs)
+    tt(T.psz0[:, 0:256], T.psz0[:, 0:256], T.zs[:, 0:256], ADD, "zs1", "psz0", 256)
+    tt(T.tr[:, 0:256], T.psz1[:, 0:256], T.zs[:, 256:512], ADD, "psz1 zs3", "t1", 256)
+    tt(T.tr[:, 256:512], T.psz0[:, 0:256], T.tr[:, 0:256], ADD, "psz0 t1", "t2", 256)
+    tt(T.tr[:, 512:640], T.tr[:, 256:384], T.tr[:, 384:512], ADD, "t2", "t3", 256)
+    tt(T.ys[:].indirect(T.yl[:]), T.tr[:, 512:576], T.tr[:, 576:640], ADD, "t3 yl", "ys", 260)
+    load("s", T.y[:], T.ys[:], "sty", 16, "ys", "y", 2.0)
+
+    queue = {"v": V, "a": S, "t": PE, "g": g, "s": SY}
+    semof = {"v": "sv", "a": "sa", "t": "st", "g": "sg"}
+    count = {"v": 0, "a": 0, "t": 0, "g": 0}
+    waited, bank = {}, {}
+    order = _arrange(ops)
+    for o in order:
+        q = o["q"]
+        if q == "x":
+            continue
+        evs = [ops[d]["ev"] for d in o["d"]]
+        banks = [k for k in o["r"] + o["w"] if k.startswith("ps")]
+        evs += [ev for k in banks for ev in bank.get(k, []) if ev[0] != semof[q]]
+        deps = {}
+        for ev in evs:
+            if ev is not None and ev[1]:
+                deps[ev[0]] = max(deps.get(ev[0], 0), ev[1])
+        for sname, val in deps.items():
+            if waited.get((q, sname), 0) < val and not (q == "g" and sname == "go"):
+                queue[q].wait_ge(T.sem[sname], val)
+                waited[(q, sname)] = val
+        if o["ev"] is None:
+            count[q] += 1
+            o["make"]().then_inc(T.sem[semof[q]], 1)
+            o["ev"] = (semof[q], count[q])
+        else:
+            o["make"]()
+        for k in banks:
+            bank.setdefault(k, []).append(o["ev"])
+
+    g.wait_ge(T.sem.csent, sum(len(e) for e in cengs))
+    g.wait_ge(T.sem.dsent, sum(len(e) for e in dengs))
+    for q in ("g", "a", "t", "v"):
+        g.wait_ge(T.sem[semof[q]], count[q])
+    g.wait_ge(T.sem.sty, 16)

@@ -1,31 +1,43 @@
+import numpy as np
 from concourse.bass import DstId, RemoteDMATransfer
 from concourse.mybir import AluOpType, ActivationFunctionType
 
 F32, I32, U16, BF, F16 = "float32", "int32", "uint16", "bfloat16", "float16"
 R, CAP = 4096, 768
-TAG = 16384
-WIN = 240
+GAP, OWNGAP = 32, 544
+BIG = GAP + 3 * (CAP + GAP) + R + OWNGAP
+STEP, LOW = 8192.0, -float(2 ** 21)
+WIN, EW = 208, 136
+SPLIT = 4096
+ACTINT = True
 
 _SB = {
-    BF: dict(xin=R, big=R + 3 * CAP, outb=3 * CAP, bo16=128, ub16=128, zm=144, rst=512, sgn=64, hr=96, ltl=384, lth=384,
-             pl=384, ph=384, cnt=56, lto=384, pr=384, nr=56, gw=1024),
-    I32: dict(idxi=256, cl=16, abz=8, pci=4, j2i=24, tb=(32, 16), ui=512, wli=4, wla=4, yp=128, npos=128, ci=144, li=96,
-              dd=96, et=384, eu=384, win=3 * WIN, wm=144, eni=128),
-    U16: dict(idxu=256, bcl=32, j2=24, pml=8, yl=4, l16=96, ls=96, lst=144, fl=128),
-    F16: dict(uf=384),
-    F32: dict(abf=8, abv=8, colf=4, cst=8, xf=144, i16=128, g16=128, pm8=8, oc0=48, oc=48, kc=48, bo32=128, u32=128, msk=128,
-              mtab=32, i2=32, nb=128, n0r=128, tagc=8, k3c=8, lf=2, cf=4, inc=4, one4=4, e1=4, st=4, st2=4, stc=8, us=384,
-              ufo=128, uso=128, key=8, wsc=4, kex=64, rk2=4, wtab=48, crep=384, wv=4, f1=32, f2=32, cg=128, bb=16, xw=16,
-              xe=256, offm=4, zn=24, nf=48, hh=48, dst=96, ep=384, em=384, ee=384, ea=384, eb=408, es=384, tsx=48, kt=32,
-              kk=32, dk=24, yo=128, en=128, epo=128, own=128, acc=640, ac2=256, ac3=128, ac4=128, df=1024, zs=512, tr=640,
-              ys=64),
+    BF: dict(xin=R, big=BIG, outb=3 * CAP, bo16=128, bon=128, eye=128, eyen=128, eye15=128, lo0=128, lo1=128, up0=128, up1=128,
+             lon=128, upn=128, zm=144, sgn=64, gl=(6, 146), zero=145, geo=387, rst=387, u16=8, gw=1024, neg=129),
+    I32: dict(idxi=256, cl=20, abz=8, pci=4, tb=512, ui=512, kwi=128, kwa=128, ci=81, lm=54, dd=54, et=384, eu=384, ee=3 * EW,
+              win=(3, WIN), wm=144, yp=128, kap=128, pos=128),
+    U16: dict(idxu=256, ucl=40, pml=8, yl=4, lr=(6, 10), ls=(6, 10), lst=144, fl=128),
+    F16: dict(uf=(4, 128), cn=(6, 146), co=387, inc=6, hr=(3, 32)),
+    F32: dict(abf=8, abv=8, a16=4, col=12, xk=152, dist=128, bo32=128, bos=128, i128=128, kwf=128, rk2=4, wc=4, i2=32, nb=128,
+              n0r=128, crep=384, wtab=48, msk=128, tab0=16, taba=16, uc0=27, kc=27, un=27, un1=27, zc=(9, 9), cf=5, st=4, bb=28,
+              xe=128, last=27, hh=27, pl=54, ep=384, ea=3 * EW, es=(3, 144), pm8=8, rkw=128, nz=8, kk=32, offb=4, nbb=20,
+              ufo=128, en=128, ye=128, yq=384, df=1024, zs=512, tr=512, ys=64),
 }
-SCRATCH = {n: ("sbuf", [128] + (list(s) if isinstance(s, tuple) else [s]), d) for d, t in _SB.items() for n, s in t.items()}
-SCRATCH.update({n: ("psum", [128, 512], F32) for n in ("psab", "psk", "psh", "psrep", "pst", "psr", "psz0", "psz1")})
-SEMAPHORES = ["sv", "sa", "st", "sg", "ldc", "lda", "ldi", "ldx", "go", "carr", "csent", "darr", "dsent", "sty"]
+SHAPE = {n: (list(s) if isinstance(s, tuple) else [s]) for t in _SB.values() for n, s in t.items()}
+SCRATCH = {n: ("sbuf", [128] + SHAPE[n], d) for d, t in _SB.items() for n in t}
+PSUM = ("psa", "psz", "psh", "psw", "pst", "psr", "ps0", "ps1")
+SHAPE.update({n: [16, 32] if n == "psw" else [512] for n in PSUM})
+SCRATCH.update({n: ("psum", [128] + SHAPE[n], F32) for n in PSUM})
+SEMAPHORES = ["sv", "sa", "st", "sg", "ldc", "lda", "ldi", "ldx", "carr", "csent", "darr", "dsent", "sty"]
 
 A = AluOpType
 AF = ActivationFunctionType
+S_ = np.s_
+PLAN = dict(small=1.5, rows=3.9, counts=2.6, sent=(2.0, 3.0, 2.5), wake=0.08, call=0.04, cycle=0.00095, gather=1.55, scatter=3.7,
+            slack=0.04, pieces=[(0, R, "a")], out="aav", halves=((0, 2), (2, 4)),
+            first=dict(n0r=3, uc0=3, i2=2, idxu=1, kwi=1, kwa=1, psh=1, outb=1),
+            scalar="abf abv a16 kwf wc uf ufo crep cf un un1 kc zc taba msk".split(), vector=["wtab"],
+            early="crep wc uf taba msk un1 kc cf".split())
 
 
 def _bits(engs):
@@ -39,7 +51,8 @@ def _peers(rank, T, topo):
     c = T.cores[rank]
     others = [q for q in range(len(T.cores)) if q != rank]
     near = [q for q in others if T.cores[q] in topo.cores_of(c)]
-    return [q for q in others if q not in near] + near
+    far = [q for q in others if q not in near]
+    return (far if rank > near[0] else far[::-1]) + near
 
 
 def _count_engines(rank, T, topo):
@@ -68,24 +81,14 @@ def _data_engines(rank, T, topo):
     return out
 
 
+def _base(rank, q):
+    return GAP + sum(R + OWNGAP if t == rank else CAP + GAP for t in range(q))
+
+
 def _arrange(ops):
-    lastw, readers = {}, {}
-    for n, o in enumerate(ops):
-        d = set()
-        for k in o["r"] + o["w"]:
-            if k in lastw:
-                d.add(lastw[k])
-        for k in o["w"]:
-            d |= set(readers.get(k, []))
-        o["d"] = d
-        for k in o["r"]:
-            readers.setdefault(k, []).append(n)
-        for k in o["w"]:
-            lastw[k] = n
-            readers[k] = []
     level = [0.0] * len(ops)
     for n in range(len(ops) - 1, -1, -1):
-        level[n] += ops[n]["c"] + ops[n]["lat"]
+        level[n] += ops[n]["c"] + ops[n]["lat"] + PLAN["first"].get(ops[n]["name"], 0.0)
         for d in ops[n]["d"]:
             level[d] = max(level[d], level[n])
     end, free, out, left = {}, {}, [], list(range(len(ops)))
@@ -93,11 +96,12 @@ def _arrange(ops):
         can = []
         for n in left:
             if all(d in end for d in ops[n]["d"]):
-                can.append((max([free.get(ops[n]["q"], 0.0)] + [end[d] for d in ops[n]["d"]]), n))
-        t0, n0 = min(can)
-        n = max((level[m], -m) for t, m in can if ops[m]["q"] == ops[n0]["q"] and t <= t0 + 0.05)[1]
+                ready = max([0.0] + [end[d] for d in ops[n]["d"]])
+                can += [(max(free.get(q, 0.0), ready), q, n) for q in ops[n]["on"]]
+        t0, q0, n0 = min(can)
+        _, n, t = max((level[m], -m, t) for t, q, m in can if q == q0 and t <= t0 + PLAN["slack"])
         n = -n
-        t = [t for t, m in can if m == n][0]
+        ops[n]["q"], ops[n]["make"] = q0, ops[n]["on"][q0]
         if ops[n]["q"] != "x":
             free[ops[n]["q"]] = t + ops[n]["c"]
         end[n] = t + ops[n]["c"] + ops[n]["lat"]
@@ -112,377 +116,387 @@ def rank_program(g, core, T, topo):
         return
     peers = _peers(me, T, topo)
     slots = peers + [me]
+    mid = 1 if 0 < me < 3 else 0
     V, S, PE, SY = g.vector, g.scalar, g.tensor, g.sync
-    ops = []
+    ops, touched = [], {}
+    CY = PLAN["cycle"]
 
-    def rec(q, make, r, w, c, lat=0.16, ev=None):
-        ops.append(dict(q=q, make=make, r=r.split(), w=w.split(), c=c, lat=lat, ev=ev))
+    def ap(name, ix=S_[:]):
+        ix = ix if isinstance(ix, tuple) else (ix,)
+        cols = np.zeros(SHAPE[name], bool)
+        cols[ix] = True
+        return T[name][(S_[:],) + ix], [(name, int.from_bytes(bytes(np.packbits(cols)), "big"))], int(cols.sum()), False
 
-    def cyc(n):
-        return 0.04 + 0.00104 * max(64, n)
+    def c1(name, j):
+        return ap(name, S_[j:j + 1])
 
-    def mm(items, r, w, n, group=True):
+    def by(win, off):
+        return win[0].indirect(off[0]), win[1] + off[1], 16 * off[2], True
+
+    def key(name):
+        return None, [(name, 1)], 0, False
+
+    def rec(q, make, r, w, c, lat=PLAN["wake"], ev=None):
+        n, d = len(ops), set()
+        r = [t for x in r if isinstance(x, tuple) for t in x[1]]
+        w = [t for x in w for t in x[1][:1]], [t for x in w for t in x[1][1:]]
+        for wr, items in ((False, r + w[1]), (True, w[0])):
+            for name, m in items:
+                d |= {k for k, km, kw in touched.get(name, []) if k != n and km & m and (wr or kw)}
+                touched.setdefault(name, []).append((n, m, wr))
+        ops.append(dict(on=make if q == "va" else {q: make}, d=d, c=c, name=w[0][0][0] if w[0] else "", lat=lat, ev=ev, banks={nm for nm, m in r + w[0] if nm in PSUM}))
+
+    def val(x):
+        return x[0] if isinstance(x, tuple) else x
+
+    def cost(o, ins, per=1.0):
+        if o[3] or ins[0][3]:
+            return 0.06 + CY * PLAN["scatter" if o[3] else "gather"] * o[2]
+        return PLAN["call"] + CY * max(64, per * o[2])
+
+    def half(*xs):
+        return 0.5 if all(SCRATCH[x[1][0][0]][2] in (BF, F16, U16) for x in xs) else 1.0
+
+    def mm(items, after=(), first=True, last=True):
         def make():
-            for k, (o, l, rh) in enumerate(items):
-                ins = PE.matmul(o, l, rh, (k == 0) or not group, (k == len(items) - 1) or not group)
+            for o, terms in items:
+                for k, (l, rh) in enumerate(terms):
+                    ins = PE.matmul(o[0], l[0], rh[0], first and k == 0, last and k == len(terms) - 1)
             return ins
-        rec("t", make, r, w, cyc(n))
+        c = sum(max(64, rh[2]) * (4 if SCRATCH[l[1][0][0]][2] == F32 else 1) for o, terms in items for l, rh in terms)
+        rec("t", make, [x for o, terms in items for t in terms for x in t] + list(after), [o for o, t in items], CY * c)
 
-    def ts1(out, in0, s1, op0, r, w, n=64):
-        rec("v", lambda: V.tensor_scalar(out, in0, s1, None, op0), r, w, cyc(n))
+    def ts(o, a, s1, op0, s2=None, op1=None, after=()):
+        more = () if op1 is None else (op1,)
+        rec("v", lambda: V.tensor_scalar(o[0], a[0], val(s1), val(s2), op0, *more), [a, s1, s2] + list(after), [o],
+            cost(o, [a], half(o, a)))
 
-    def ts2(out, in0, s1, s2, op0, op1, r, w, n=64):
-        rec("v", lambda: V.tensor_scalar(out, in0, s1, s2, op0, op1), r, w, cyc(n))
+    def tt(o, a, b, op):
+        both = a[1][0][0] not in PSUM and b[1][0][0] not in PSUM
+        rec("v", lambda: V.tensor_tensor(o[0], a[0], b[0], op), [a, b], [o], cost(o, [a], 2.0 if both else 1.0))
 
-    def tt(out, in0, in1, o, r, w, n=64):
-        rec("v", lambda: V.tensor_tensor(out, in0, in1, o), r, w, cyc(n))
+    def cp(o, a, after=()):
+        rec("v", lambda: V.tensor_copy(o[0], a[0]), [a] + list(after), [o], cost(o, [a], half(o, a)))
 
-    def cp(out, in_, r, w, n=64):
-        rec("v", lambda: V.tensor_copy(out, in_), r, w, cyc(n))
+    def scan(o, d0, d1, o0, o1):
+        rec("v", lambda: V.tensor_tensor_scan(o[0], d0[0], d1[0], 0.0, o0, o1), [d0, d1], [o], cost(o, [d0], half(o, d0, d1)))
 
-    def scan(out, d0, d1, o0, o1, r, w, n=64):
-        rec("v", lambda: V.tensor_tensor_scan(out, d0, d1, 0.0, o0, o1), r, w, cyc(n))
+    def act(o, a, func=AF.Identity, scale=1.0, bias=0.0, accum=None, after=(), who="va"):
+        kw = {} if func == AF.Copy else dict(scale=val(scale), bias=val(bias))
+        if accum:
+            kw["accum_out"] = accum[0]
+        on = dict(a=lambda: S.activation(o[0], a[0], func, **kw))
+        if func == AF.Copy:
+            on["v"] = lambda: V.tensor_copy(o[0], a[0])
+        if func == AF.Identity:
+            on["v"] = lambda: V.tensor_scalar(o[0], a[0], val(scale), val(bias), A.mult, A.add)
+        who = "a" if o[1][0][0] in PLAN["scalar"] else "v" if o[1][0][0] in PLAN["vector"] else who
+        rec("va", {q: on[q] for q in who if q in on}, [a, scale, bias] + list(after), [o] + ([accum] if accum else []), cost(o, [a]))
 
-    def act(out, in_, r, w, n=64, func=AF.Identity, **kw):
-        rec("a", lambda: S.activation(out, in_, func, **kw), r, w, cyc(n))
+    def iota(o, pattern, base=0, cm=0, late=True):
+        kw = {} if SCRATCH[o[1][0][0]][2] == I32 else dict(allow_small_or_imprecise_dtypes=True)
+        rec("g", lambda: g.iota(o[0], pattern, base, cm, **kw), [key("go")] if late else [], [o], 0.13 + 2 * CY * o[2])
 
-    def iota(out, pattern, base, cm, w, n, r="go", whole=False):
-        kw = {} if whole else dict(allow_small_or_imprecise_dtypes=True)
-        rec("g", lambda: g.iota(out, pattern, base, cm, **kw), r, w, 0.13 + 0.0021 * n)
+    def fill(o, v, who="g"):
+        if who == "g":
+            iota(o, [[0, o[2]]], int(v))
+        else:
+            rec("v", lambda: V.memset(o[0], v), [], [o], cost(o, [o], half(o)))
 
-    def fill(out, n, val, w, whole=False):
-        iota(out, [[0, n]], val, 0, w, n, whole=whole)
+    def band(o, src, step, cmp):
+        rec("g", lambda: g.affine_select(o[0], src[0], [[step, 128]], cmp, 0.0, 0, -step), [key("go"), src], [o], 0.42)
 
-    def load(q, out, in_, sem, val, r, w, lat):
-        rec(q, lambda: (SY if q == "s" else S).dma_start(out, in_).then_inc(T.sem[sem], 16), r, w, 0.05, lat, (sem, val))
+    def load(q, out, in_, sem, v, r, w, lat):
+        rec(q, lambda: (SY if q == "s" else S).dma_start(out, in_).then_inc(T.sem[sem], 16), r, w, 0.05, lat, (sem, v))
 
-    def suffix(ps, n, r, w):
-        mm([(ps[:, 0:48], T.ub16[:], n[:, 0:48])] + [(ps[:, 0:48], T.bo16[:], n[:, d:d + 48]) for d in range(1, 8)],
-           "ub16 bo16 " + r, w, 512)
-
-    SHR, AND, MUL, ADD, SUB = A.arith_shift_right, A.bitwise_and, A.mult, A.add, A.subtract
+    SHR, AND, MUL, ADD, SUB, MAX = A.arith_shift_right, A.bitwise_and, A.mult, A.add, A.subtract, A.max
     cengs, dengs = _count_engines(me, T, topo), _data_engines(me, T, topo)
     carr = sum(len(_count_engines(q, T, topo)[_peers(q, T, topo).index(me)]) for q in peers)
     darr = sum(len(_data_engines(q, T, topo)[_peers(q, T, topo).index(me)]) for q in peers)
-    mine = T.cl[:, 4 * me:4 * me + 4]
+    mine = ap("cl", S_[4 + 4 * me:8 + 4 * me])
+    b0 = _base(me, me)
+    tofloat = act if ACTINT else cp
 
-    load("s", mine, T.counts[:], "ldc", 16, "", "clme q1", 2.0)
-    rec("v", lambda: V.memset(T.abz[:], 0), "", "abz", 0.1)
-    load("s", T.abz[0:128:16, :], T.ab[:], "lda", 16, "", "abz", 2.0)
-    load("a", T.idxi[:], T.idx[:], "ldi", 16, "", "idxi", 2.2)
-    rec("x", None, "", "q2", 0.0, 0.4)
-    load("s", T.xin[:, 0:R // 2], T.x[:, 0:R // 2], "ldx", 16, "q2", "xa", 3.5)
+    load("s", mine[0], T.counts[:], "ldc", 16, [], [mine], PLAN["small"])
+    rec("v", lambda: V.memset(T.abz[:], 0), [], [ap("abz")], 0.1)
+    load("s", T.abz[0:128:16, :], T.ab[:], "lda", 16, [], [ap("abz")], PLAN["small"])
+    load("a", T.idxi[:], T.idx[:], "ldi", 16, [], [ap("idxi")], PLAN["small"] + 0.2)
+    rec("x", None, [], [key("behind")], 0.0, 0.3)
+    load("s", T.xin[:], T.x[:], "ldx", 16, [key("behind")], [ap("xin")], PLAN["rows"])
 
     def send_counts():
         trs = []
         for q, e in zip(peers, cengs):
             rid, pid = topo.addr(T.cores[q], core)
             trs.append(RemoteDMATransfer(dst_ids=[DstId(rid=rid, pnc=pid)], dma_engine_mask=_bits(e), remote_sem=T.sem.carr,
-                                         src=mine, dst=mine))
+                                         src=mine[0], dst=mine[0]))
         g.remote_dma_fused(trs, local_sem=T.sem.csent)
-        g.sem_inc(T.sem.go, 1)
 
-    rec("g", send_counts, "clme", "go", 0.3, 0.1, ("go", 1))
-    rec("x", None, "go", "clfar", 0.0, 3.5, ("carr", carr))
-    load("s", T.xin[:, R // 2:R], T.x[:, R // 2:R], "ldx", 32, "go", "xin", 3.5)
+    rec("g", send_counts, [mine], [key("go")], 0.3, 0.0, ("", 0))
+    rec("x", None, [key("go")], [ap("cl", S_[4 + 4 * q:8 + 4 * q]) for q in peers], 0.0, PLAN["counts"], ("carr", carr))
 
-    iota(T.pci[:, 0:1], [[0, 1]], 0, 1, "p", 1, "", True)
-    iota(T.g16[:], [[1, 8], [0, 16]], 0, 0, "g16", 128, "")
-    iota(T.xf[:], [[1, 144]], 0, 0, "xf", 144, "")
-    iota(T.i16[:], [[0, 8], [1, 16]], 0, 0, "i16", 128, "")
-    iota(T.n0r[:], [[16, 8], [128, 16]], 0, 0, "n0r", 128)
-    iota(T.oc0[:], [[0, 3], [16, 16]], 0, 0, "oc0", 48)
-    iota(T.pm8[:], [[1, 2], [16, 2], [8, 2]], 0, 0, "pm8", 8)
-    iota(T.i2[:], [[0, 2], [2, 16]], -15, 0, "i2", 32)
-    iota(T.j2i[:], [[1, 12], [0, 2]], 0, 0, "j2i", 24, whole=True)
-    rec("g", lambda: g.affine_select(T.u32[:], T.bo32[:], [[-1, 128]], A.is_ge, 0.0, 0, 1), "go bo32", "u32", 0.44)
-    fill(T.cnt[:], 56, 0, "cnt0")
-    fill(T.nr[:], 56, 0, "nr0")
-    fill(T.xw[:], 16, 0, "xw0")
-    fill(T.ci[:, 96:144], 48, 0, "rho0", True)
-    fill(T.kk[:, 8 * me:8 * me + 8], 8, 0, "kk%d" % me)
+    def xf(a, b):
+        return ap("xk", S_[8 + a:8 + b])
+
+    def bcl(a, b):
+        return ap("ucl", S_[8 + a:8 + b])
+
+    iota(c1("pci", 0), [[0, 1]], 0, 1, False)
+    iota(xf(0, 144), [[1, 144]], 0, 0, False)
+    iota(ap("i128", S_[0:64]), [[0, 4], [1, 16]], 0, 0, False)
+    iota(ap("xk", S_[0:8]), [[0, 2], [slots[2] - slots[0], 2], [slots[1] - slots[0], 2]], slots[0], 0, False)
+    for k, m in enumerate((15, 112, 3)):
+        ts(c1("pci", k + 1), c1("pci", 0), m, AND)
+    cp(ap("col", S_[0:4]), ap("pci"))
+    part, lane, g16, l3 = c1("col", 0), c1("col", 1), c1("col", 2), c1("col", 3)
+    act(c1("col", 4), g16, scale=-1.0, bias=-7.5)
+    act(ap("dist"), xf(0, 128), AF.Abs, bias=c1("col", 4))
+    ts(ap("bo32"), ap("dist"), 8.0, A.is_lt)
+    act(ap("bo16"), ap("bo32"))
+    act(ap("bon"), ap("bo32"), scale=-1.0)
+    act(ap("bos"), ap("bo32"), scale=1.0 / 65536)
+    ts(ap("eye"), xf(0, 128), part, A.is_equal)
+    act(ap("eyen"), ap("eye"), scale=-1.0)
+    act(ap("eye15"), ap("eye"), scale=15.0)
+    act(c1("col", 5), lane, scale=128.0)
+    act(ap("nb"), xf(0, 128), bias=c1("col", 5))
+    act(ap("i128", S_[64:128]), xf(0, 64), scale=0.0, bias=lane)
+    cp(ap("ucl"), ap("xk", S_[0:40]))
+    act(c1("col", 6), g16, bias=15.0)
+    ts(ap("zm"), xf(0, 144), c1("col", 6), A.is_equal)
+    act(c1("col", 10), lane, scale=-1.0 / 16, bias=-2048.0)
+    iota(ap("i2"), [[0, 2], [-2, 16]], 15)
+    iota(ap("n0r"), [[16, 8], [128, 16]])
+    band(ap("lo0"), ap("bo16"), 1, A.is_gt)
+    band(ap("up0"), ap("bo16"), -1, A.is_ge)
+    band(ap("lo1"), ap("bo16"), 1, A.is_ge)
+    band(ap("up1"), ap("bo16"), -1, A.is_gt)
+    iota(ap("uc0"), [[0, 3], [16, 9]])
+    act(ap("un"), ap("uc0"), bias=lane)
+    act(ap("kc"), ap("un"), bias=64.0)
+    act(ap("zc", S_[3:6]), ap("un"), scale=-16.0 * (1 + mid), bias=-1024.0)
+    act(ap("zc", S_[0:3]), ap("un"), scale=-16.0 * (1 + mid), bias=-1024.0 - 16 * mid)
+    act(ap("un1"), ap("un"), bias=1.0)
+    fill(ap("zc", S_[6:9, 8:9]), 0)
+    ts(ap("msk", S_[0:64]), ap("i128", S_[0:64]), lane, A.is_equal, 1.0 / 1024, MUL)
+    act(ap("msk", S_[64:128]), ap("msk", S_[0:64]), scale=1024.0)
+    ts(ap("tab0"), xf(0, 16), lane, A.is_le)
+    act(ap("taba"), ap("tab0"), scale=STEP - LOW, bias=LOW)
+    fill(ap("cl", S_[0:4]), 0)
+    fill(c1("cf", 0), 0, "v")
+    fill(ap("zero"), 0, "v")
+    fill(ap("neg"), -STEP)
+    fill(ap("gl", S_[:, 0:1]), 0)
+    fill(ap("gl", S_[:, 129:145]), 1)
+    fill(ap("ee", S_[0:3 * EW:EW]), LOW)
+    fill(ap("ea", S_[128:3 * EW:EW]), LOW)
+    fill(ap("es", S_[:, 129:144]), 0)
+    fill(ap("win", S_[:, 0:48]), 0)
+
+    tofloat(ap("abf"), ap("abz"))
+    mm([(ap("psa", S_[0:8]), [(ap("bo32"), ap("abf"))])])
+    act(ap("abv"), ap("psa", S_[0:8]))
+    ac = [c1("abv", 2 * q) for q in slots]
+    bc = [c1("abv", 2 * q + 1) for q in slots]
+    for k in range(4):
+        ts(ap("tb", S_[128 * k:128 * k + 128]), ap("nb"), ac[k], MUL, bc[k], ADD)
+    for a, b in PLAN["halves"]:
+        ts(ap("ui", S_[128 * a:128 * b]), ap("tb", S_[128 * a:128 * b]), 2, SHR, 1023, AND)
+        act(ap("uf", S_[a:b]), ap("ui", S_[128 * a:128 * b]), scale=1.0 / 1024)
     for k in range(3):
-        fill(T.eb[:, 136 * k:136 * k + 1], 1, 0, "eb0%d" % k)
-        fill(T.win[:, WIN * k:WIN * k + 48], 48, 0, "w%d" % k, True)
-    rec("v", lambda: V.memset(T.rst[:], 1.0), "", "rst", cyc(256))
-    rec("v", lambda: V.memset(T.rst[:, 0:512:16], 0.0), "", "rst", cyc(64))
-    rec("v", lambda: V.memset(T.one4[:], 1.0), "", "one4", cyc(64))
-    lane, grp = T.colf[:, 1:2], T.colf[:, 2:3]
-    ts1(T.pci[:, 1:2], T.pci[:, 0:1], 15, AND, "p", "lanei")
-    ts1(T.pci[:, 2:3], T.pci[:, 0:1], 4, SHR, "p", "grpi")
-    ts1(T.pci[:, 3:4], T.pci[:, 1:2], 2, SHR, "lanei", "l2")
-    cp(T.colf[:, 0:3], T.pci[:, 0:3], "p lanei grpi", "colf")
-    act(T.cst[:, 0:1], lane, "colf", "lane128", scale=128.0)
-    act(T.cst[:, 1:2], grp, "colf", "c15", scale=16.0, bias=15.0)
-    act(T.cst[:, 2:3], lane, "colf", "lanetag", scale=float(TAG), bias=float(4096 + 2 ** 23))
-    act(T.cst[:, 4:5], lane, "colf", "lane4", scale=4.0)
-    act(T.cst[:, 5:6], lane, "colf", "lane32", scale=32.0)
-    act(T.nb[:], T.xf[:, 0:128], "xf lane128", "nb", 128, bias=T.cst[:, 0:1])
-    act(T.tagc[:], T.xf[:, 0:8], "xf lanetag", "tagc", scale=float(16 * TAG), bias=T.cst[:, 2:3])
-    act(T.oc[:], T.oc0[:], "oc0 colf", "oc", bias=lane)
-    act(T.kc[:], T.oc[:], "oc", "kc", bias=64.0)
-    act(T.bo16[:], T.bo32[:], "bo32", "bo16", 128)
-    act(T.ub16[:], T.u32[:], "u32", "ub16", 128)
-    ts1(T.bo32[:], T.g16[:], grp, A.is_equal, "g16 colf", "bo32", 128)
-    ops.insert(0, ops.pop())
-    ts1(T.msk[:], T.i16[:], lane, A.is_equal, "i16 colf", "msk", 128)
-    cp(T.bcl[:], T.xf[:, 0:32], "xf", "bcl")
-    ts1(T.zm[:], T.xf[:], T.cst[:, 1:2], A.is_equal, "xf c15", "zm", 144)
-    ts1(T.mtab[:], T.xf[:, 0:32], lane, A.is_le, "xf colf", "mtab")
-    cp(T.j2[:], T.j2i[:], "j2i", "j2")
-    ts2(T.lf[:, 0:1], T.pci[:, 3:4], -126.0, T.cst[:, 5:6], MUL, ADD, "l2 lane32", "lf0")
-    ts1(T.yl[:], T.xf[:, 0:4], T.cst[:, 4:5], ADD, "xf lane4", "yl")
-    ts1(T.pml[:], T.pm8[:], T.lf[:, 0:1], ADD, "pm8 lf0", "pml")
-    base = {q: float(R + CAP * peers.index(q) + CAP + 15) for q in peers}
-    if me != 3:
-        act(T.lf[:, 1:2], lane, "colf", "lf1", scale=16.0, bias=base[3] - 2048.0)
-        act(T.k3c[:], T.xf[:, 0:8], "xf lf1", "k3c", scale=256.0, bias=T.lf[:, 1:2])
-    made = {k: o for o in ops for k in o["w"]}
-    head = []
-
-    def first(o):
-        if not any(o is h for h in head):
-            for k in o["r"]:
-                first(made[k])
-            head.append(o)
-
-    for o in list(ops):
-        first(o)
-    ops[:] = head
-
-    cp(T.abf[:], T.abz[:], "abz", "abf")
-    mm([(T.psab[:, 0:8], T.bo32[:], T.abf[:])], "bo32 abf", "psab", 256)
-    cp(T.abv[:], T.psab[:, 0:8], "psab", "abv")
-    cp(T.cf[:], mine, "clme", "cf")
-    scan(T.inc[:], T.one4[:], T.cf[:], MUL, ADD, "one4 cf", "inc")
-    mm([(T.psr[:, 0:4], T.u32[:], T.inc[:])], "u32 inc", "psr", 256)
-    tt(T.e1[:], T.inc[:], T.cf[:], SUB, "inc cf", "e1")
-    ts2(T.st[:], T.e1[:], T.psr[:, 3:4], float(R), SUB, ADD, "e1 psr", "st")
-    tt(T.stc[:, 0:8:2], T.tagc[:, 0:8:2], T.st[:], ADD, "tagc st", "stc0")
-    tt(T.stc[:, 1:8:2], T.tagc[:, 1:8:2], T.st[:], ADD, "tagc st", "stc1")
-
-    def ac(q):
-        return T.abv[:, 2 * q:2 * q + 1]
-
-    def bc(q):
-        return T.abv[:, 2 * q + 1:2 * q + 2]
-
+        act(ap("crep", S_[128 * k:128 * k + 128]), ap("n0r"), scale=ac[k], bias=bc[k])
+    act(ap("a16"), ap("psa", S_[0:8:2]), scale=16.0, bias=1.0)
+    tt(ap("kwi"), by(ap("a16"), ap("ucl", S_[0:8])), ap("i128"), MUL)
+    ts(ap("kwa"), ap("kwi"), 65535, AND)
+    tofloat(ap("kwf"), ap("kwa"))
+    act(ap("wc"), ap("kwf", S_[64:128:16]), scale=1.0 / 16, bias=c1("col", 10))
+    for k in range(4):
+        c = S_[16 * k:16 * k + 16]
+        act(ap("sgn", c), ap("kwf", c), AF.Sign, -1.0, c1("kwf", 64 + 16 * k), c1("rk2", k))
     for k in range(3):
-        ts2(T.tb[:, k:24:3, :], T.nb[:], ac(slots[k]), bc(slots[k]), MUL, ADD, "nb abv", "tb%d" % k, 128)
-        act(T.crep[:, 128 * k:128 * k + 128], T.n0r[:], "n0r abv", "crep%d" % k, 128, scale=ac(slots[k]), bias=bc(slots[k]))
-    ts2(T.tb[:, 24:32, :], T.nb[:], ac(me), bc(me), MUL, ADD, "nb abv", "tb3", 128)
-    ts2(T.ui[:, 0:384], T.tb[:, 0:24, :], 2, 1023, SHR, AND, "tb0 tb1 tb2", "ui", 384)
-    ts2(T.ui[:, 384:512], T.tb[:, 24:32, :], 2, 1023, SHR, AND, "tb3", "uio", 128)
-    ts1(T.uf[:], T.ui[:, 0:384], 1.0 / 1024, MUL, "ui", "uf", 384)
-    ts1(T.ufo[:], T.ui[:, 384:512], 1.0 / 1024, MUL, "uio", "ufo", 128)
-    ts1(T.wli[:], T.abv[:, 0:8:2], lane, MUL, "abv colf", "wli")
-    ts1(T.wla[:], T.wli[:], 4095, AND, "wli", "wla")
-    ts2(T.key[:, 0:4], T.wla[:], 16.0, lane, MUL, ADD, "wla colf", "key")
-    ts2(T.wsc[:], T.wla[:], 1.0 / 4096, -1.0, MUL, ADD, "wla", "wsc")
-    tt(T.kex[:], T.key[:, 0:4].indirect(T.bcl[:, 0:4]), T.msk[:, 0:64], MUL, "key bcl msk", "kex", 120)
-    mm([(T.psk[:, 0:64], T.bo32[:], T.kex[:]), (T.psk[:, 64:68], T.bo32[:], T.wsc[:])], "bo32 kex wsc", "psk", 512, False)
-    for q in slots:
-        act(T.sgn[:, 16 * q:16 * q + 16], T.psk[:, 16 * q:16 * q + 16], "psk key", "sgn%d rk%d" % (q, q),
-            func=AF.Sign, scale=-1.0, bias=T.key[:, q:q + 1], accum_out=T.rk2[:, q:q + 1])
-    act(T.wv[:], T.psk[:, 64:68], "psk", "wv", scale=-1.0, bias=0.25)
-    for k in range(3):
-        ts2(T.hr[:, k:96:3], T.i2[:], T.rk2[:, slots[k]:slots[k] + 1], lane, A.is_equal, MUL, "i2 colf rk%d" % slots[k],
-            "hr%d" % k)
-    mm([(T.psh[:, 0:48], T.zm[:, 15 - k:143 - k], T.hr[:, 3 * k:3 * k + 48]) for k in range(16)], "zm hr0 hr1 hr2", "psh", 1024)
-    for k in range(3):
-        ts1(T.wtab[:, 16 * k:16 * k + 16], T.psh[:, k:48:3], ac(slots[k]), MUL, "psh abv", "wtab%d" % k)
-    mm([(T.psab[:, 16 * k:16 * k + 16], T.bo16[:], T.sgn[:, 16 * me:16 * me + 16]) for k in range(8)],
-       "bo16 sgn%d" % me, "psab", 512, False)
-    scan(T.us[:], T.rst[:, 0:384], T.uf[:], MUL, ADD, "rst uf", "us", 384)
-    scan(T.uso[:], T.rst[:, 0:128], T.ufo[:], MUL, ADD, "rst ufo", "uso", 128)
-    for k in range(3):
-        ts2(T.f1[:, k:24:3], T.uf[:, 16 * k:384:48], -16.0, T.wv[:, slots[k]:slots[k] + 1], MUL, ADD, "uf wv", "f1%d" % k)
-    tt(T.f2[:, 0:24], T.us[:, 15:384:16], T.f1[:, 0:24], ADD, "us f10 f11 f12", "z")
-    ts2(T.f1[:, 24:32], T.ufo[:, 0:128:16], -16.0, T.wv[:, me:me + 1], MUL, ADD, "ufo wv", "f13")
-    tt(T.f2[:, 24:32], T.uso[:, 15:128:16], T.f1[:, 24:32], ADD, "uso f13", "zo")
+        ts(ap("hr", S_[k]), ap("i2"), c1("rk2", k), A.is_equal, c1("wc", k), MUL)
+    mm([(ap("psh", S_[0:48]), [(ap("zm", S_[15 - k:143 - k]), ap("hr", S_[:, 15 - k:31 - k])) for k in range(16)])])
+    act(ap("wtab"), ap("psh", S_[0:48]), bias=2048.0)
+    mm([(ap("psz", S_[0:32]), [(ap("bos"), ap("kwf", S_[64:128:2]))])], last=False)
+    mm([(ap("psz", S_[0:32]), [(ap("eyen" if i else "eye15"), ap("uf", S_[:, i:128:16])) for i in range(16)])], first=False)
+    cp(ap("zc", S_[6:9, 0:8]), ap("psz", S_[0:24]))
+    tofloat(ap("cf", S_[1:5]), mine)
+    scan(ap("inc", S_[0:5]), ap("cf"), ap("zero", S_[0:5]), ADD, ADD)
+    mm([(c1("psr", 64), [(ap("lo0"), c1("inc", 4))])])
+    off = ap("bb", S_[24:28])
+    ts(ap("st") if me else off, ap("inc", S_[0:4]), c1("psr", 64), ADD, -0.5 + 2.0 ** -11, ADD)
 
-    cp(T.idxu[:], T.idxi[:], "idxi", "idxu", 256)
-    late = "crep0 crep1 crep2 wv oc kc ub16 " + " ".join("rk%d" % q for q in slots)
-    act(T.big[:, 0:R], T.xin[:].indirect(T.idxu[:]), "xin idxu " + late, "xs", 6400, func=AF.Copy)
+    cp(ap("idxu"), ap("idxi"))
+    for a, b, who in PLAN["pieces"]:
+        act(ap("big", S_[b0 + a:b0 + b]), by(ap("xin"), ap("idxu", S_[a // 16:b // 16])), AF.Copy, who=who,
+            after=[ap(n) for n in PLAN["early"]] + [ap("rk2", S_[0:3]), ap("zc", S_[0:6])])
 
-    cq = [T.cl[:, 4 * q:4 * q + 4] for q in range(4)]
-    bnd = {1: T.bb[:, 0:4], 2: T.bb[:, 4:8], 3: T.bb[:, 8:12]}
-    tt(bnd[2], cq[0], cq[1], ADD, "clme clfar", "b2")
-    tt(T.bb[:, 12:16], cq[2], cq[3], ADD, "clme clfar", "b23")
-    cp(bnd[1], cq[0], "clme clfar", "b1")
-    tt(T.xw[:, 0:4], bnd[2], T.bb[:, 12:16], ADD, "xw0 b2 b23", "size")
-    tt(bnd[3], bnd[2], cq[2], ADD, "b2 clme clfar", "b3")
-    lo, hi = me, me + 1
-
-    def under(out, nout, b, key):
-        for j in range(4):
-            ts2(out[:, 96 * j:96 * j + 96], T.uf[:, 96 * j:96 * j + 96], T.xw[:, j:j + 1], bnd[b][:, j:j + 1], MUL, A.is_lt,
-                "uf size b%d" % b, "%s%d" % (key, j))
-        scan(nout[:], T.rst[:, 0:384], out[:], MUL, ADD, "rst #0 #1 #2 #3".replace("#", key), "n" + key, 192)
-
-    for hh in range(2):
-        o, s = T.xw[:, 8 + hh:16:2], T.stc[:, hh:8:2]
-        if me == 0:
-            cp(o, s, "xw0 stc%d" % hh, "off%d" % hh)
-        else:
-            tt(o, s, bnd[lo], SUB, "xw0 stc%d b%d" % (hh, lo), "off%d" % hh)
-    if me != 0:
-        under(T.ltl, T.pl, lo, "lo")
-    if me != 3:
-        under(T.lth, T.ph, hi, "hi")
-    for k in range(3):
-        o, e = T.cnt[:, 16 * k:16 * k + 8], slice(16 * k + 15, 384, 48)
-        if me == 0:
-            cp(o, T.ph[:, e], "cnt0 nhi", "cnt%d" % (k + 1))
-        elif me == 3:
-            ts2(o, T.pl[:, e], -1.0, 16.0, MUL, ADD, "cnt0 nlo", "cnt%d" % (k + 1))
-        else:
-            tt(o, T.ph[:, e], T.pl[:, e], SUB, "cnt0 nlo nhi", "cnt%d" % (k + 1))
-    suffix(T.pst, T.cnt, "cnt1 cnt2 cnt3", "pst")
-    tt(T.xe[:, 0:128], T.xw[:].indirect(T.j2[:, 0:8]), T.msk[:], MUL, "size off0 off1 j2 msk", "xe0", 220)
-    tt(T.xe[:, 128:256], T.xw[:].indirect(T.bcl[:, 8:16]), T.msk[:], MUL, "size off0 off1 bcl msk", "xe1", 220)
-    mm([(T.psrep[:, 0:256], T.bo32[:], T.xe[:])], "bo32 xe0 xe1", "psrep", 1024)
-
-    ts2(T.ci[:, 48:96], T.pst[:, 0:48], -1.0, float(CAP), MUL, ADD, "pst", "ci")
-    if me == 0:
-        zn = T.f2
-    else:
-        zn = T.zn
-        tt(T.zn[:], T.pl[:, 15:384:16], T.f2[:, 0:24], ADD, "nlo z", "zn")
-    tt(T.ci[:, 0:48], T.ci[:, 48:96], T.cnt[:, 0:48], ADD, "ci cnt1 cnt2 cnt3", "ce", 96)
-    for k in range(3):
-        tt(T.ci[:, 96 + 16 * k:104 + 16 * k], zn[:, k:24:3], T.pst[:, 16 * k:16 * k + 8], ADD, "rho0 z zn pst", "rho%d" % (k + 1))
-    ts1(T.li[:], T.ci[:, 48:144], 15, AND, "ci rho1 rho2 rho3", "li", 96)
-    cp(T.l16[:], T.li[:], "li", "l16", 96)
-    ts1(T.dd[:], T.ci[:, 0:96], 4, SHR, "ci ce", "dd", 96)
-    tt(T.nf[:], T.dd[:, 0:48], T.dd[:, 48:96], A.is_equal, "dd", "nf", 96)
-    tt(T.hh[:], T.nf[:], T.kc[:], MUL, "nf kc", "hh", 96)
-    tt(T.dst[:, 0:48], T.hh[:], T.dd[:, 48:96], ADD, "hh dd", "dst", 96)
-    tt(T.dst[:, 48:96], T.oc[:], T.hh[:], SUB, "hh oc", "lbf", 96)
-    cp(T.ls[:], T.dst[:], "dst lbf", "ls", 96)
-
-    def chain(k):
-        c = slice(128 * k, 128 * k + 128)
-        u = slice(16 * k, 16 * k + 8)
-        u2 = slice(48 + 16 * k, 56 + 16 * k)
-        m = slice(48 * k, 48 * k + 48)
-        e0, w0, q = 136 * k, WIN * k, peers[k]
-
-        def n(s):
-            return s.replace("#", str(k))
-        tt(T.et[:, c], T.wtab[:, 16 * k:16 * k + 16].indirect(T.l16[:, u2]), T.crep[:, c], ADD, n("wtab# l16 crep#"), n("et#"), 220)
-        ts2(T.eu[:, c], T.et[:, c], 2, 1023, SHR, AND, n("et#"), n("eu#"), 128)
-        tt(T.ep[:, c], T.eu[:, c], T.psrep[:, 0:128], MUL, n("eu# psrep"), n("ep#"), 128)
-        act(T.em[:, c], T.ep[:, c], n("ep#"), n("em#"), 128, scale=1.0 / 1024, bias=-0.5 + 2.0 ** -11)
-        tt(T.ee[:, c], T.em[:, c], T.psrep[:, 128:256], ADD, n("em# psrep"), n("ee#"), 128)
-        tt(T.ea[:, c], T.mtab[:].indirect(T.l16[:, u]), T.ee[:, c], MUL, n("mtab l16 ee#"), n("ea#"), 220)
-        act(T.eb[:, e0 + 1:e0 + 129], T.ee[:, c].indirect(T.ls[:, u2]), n("ls ee#"), n("ebb#"), 220, func=AF.Copy)
-        scan(T.es[:, c], T.eb[:, e0:e0 + 128], T.ea[:, c], A.max, A.max, n("eb0# ebb# ea#"), n("es#"), 128)
-        cp(T.win[:, w0:w0 + WIN].indirect(T.ls[:, u]), T.es[:, c], n("ls es#"), n("w#"), 490)
-        ts1(T.wm[:, m], T.win[:, w0:w0 + 48], R - 1, AND, n("w#"), n("wm#"))
-        cp(T.lst[:, m], T.wm[:, m], n("wm#"), n("lst#"))
-        src = T.outb[:, CAP * k:CAP * k + CAP]
-        act(src, T.big[:, 0:R].indirect(T.lst[:, m]), n("xs lst#"), n("out#"), 1220, func=AF.Copy)
-        rid, pid = topo.addr(T.cores[q], core)
-        at = R + CAP * _peers(q, T, topo).index(me)
-        rec("g", lambda: g.remote_dma(T.big[:, at:at + CAP], src, T.sem.darr, T.sem.dsent, pid, rid, _bits(dengs[k])),
-            n("out#") + (" sent0" if k == 1 else ""), n("sent#"), 0.3, (2.0, 4.5, 3.5)[k], ("", 0))
-
-    for k in range(3):
-        chain(k)
-    rec("x", None, "sent0 sent1 sent2", "land", 0.0, 0.0, ("darr", darr))
-
-    act(T.cg[:], T.psab[:, 0:128], "psab xs", "cg", 128, scale=0.5, bias=7.5)
-    ts1(T.st2[:], T.st[:], -0.5 + 2.0 ** -11, ADD, "st", "st2")
-    if me == 0:
-        offm, offk = T.st2, "st2"
-    else:
-        tt(T.offm[:], T.st2[:], bnd[lo], SUB, "st2 b%d" % lo, "offm")
-        offm, offk = T.offm, "offm"
+    tt(ap("bb", S_[0:16]), ap("cl", S_[0:16]), ap("cl", S_[4:20]), ADD)
+    tt(ap("bb", S_[16:24]), ap("bb", S_[0:8]), ap("bb", S_[8:16]), ADD)
+    bnd = {1: 0, 2: 4, 3: 16}
     for j in range(4):
-        c = slice(32 * j, 32 * j + 32)
-        act(T.yo[:, c], T.ufo[:, c], "ufo size xs", "yo%d" % j, scale=T.xw[:, j:j + 1])
-        act(T.en[:, c], T.ufo[:, c], "ufo size xs " + offk, "en%d" % j, scale=T.xw[:, j:j + 1], bias=offm[:, j:j + 1])
-
-    def lto(b):
-        return T.lto[:, 128 * b - 128:128 * b]
-
-    for b in (1, 2, 3):
-        tt(lto(b), T.bb[:].indirect(T.j2[:, 8 * b - 8:8 * b]), T.yo[:], A.is_gt, "b1 b2 b3 b23 j2 yo0 yo1 yo2 yo3", "lt%d" % b, 220)
-    scan(T.pr[:], T.rst[:, 0:384], T.lto[:], MUL, ADD, "rst lt1 lt2 lt3", "pr", 192)
-    for b in (1, 2, 3):
-        cp(T.nr[:, 16 * b - 16:16 * b - 8], T.pr[:, 128 * b - 113:128 * b:16], "nr0 pr", "nr%d" % b)
-    suffix(T.psr, T.nr, "nr1 nr2 nr3", "psr")
-    tt(T.yp[:], T.f2[:, 24:32].indirect(T.bcl[:, 0:8]), T.cg[:], ADD, "zo bcl cg", "yp", 220)
-    ts1(T.npos[:], T.yp[:], 15, AND, "yp", "npos", 128)
-    cp(T.eni[:], T.en[:], "en0 en1 en2 en3", "eni", 128)
-    tt(T.tsx[:], T.psr[:, 0:48], T.nr[:, 0:48], SUB, "psr nr1 nr2 nr3", "tsx")
-    if me != 0:
-        ts2(T.kk[:, 0:8], T.psr[:, 0:8], -1.0, base[0], MUL, ADD, "psr", "kk0")
-    tt(T.epo[:], T.eni[:], T.npos[:], ADD, "eni npos", "epo", 256)
-    for q in (1, 2):
-        if q != me:
-            tt(T.kt[:, 8 * q:8 * q + 8], T.tsx[:, 16 * q - 16:16 * q - 8], T.psr[:, 16 * q:16 * q + 8], SUB, "tsx psr", "kt%d" % q)
-            ts1(T.kk[:, 8 * q:8 * q + 8], T.kt[:, 8 * q:8 * q + 8], base[q], ADD, "kt%d" % q, "kk%d" % q)
-    if me != 3:
-        tt(T.kk[:, 24:32], T.tsx[:, 32:40], T.k3c[:], ADD, "tsx k3c", "kk3")
-    if me == 0:
-        tt(T.psz0[:, 0:128], T.epo[:], lto(1), MUL, "epo lt1", "psz0", 256)
+        c = S_[32 * j + 1:32 * j + 33]
+        u = ap("uf", S_[0:3, 32 * j:32 * j + 32])
+        if me != 0:
+            ts(ap("gl", S_[0:3, c]), u, c1("bb", 20 + j), MUL, c1("bb", bnd[me] + j), A.is_ge)
+        if me != 3:
+            ts(ap("gl", S_[3:6, c]), u, c1("bb", 20 + j), MUL, c1("bb", bnd[me + 1] + j), A.is_lt)
+    for k in range(3):
+        scan(ap("cn", S_[k, 0:145]), ap("gl", S_[k if me else 3 + k, 0:145]), ap("gl", S_[3 + k, 0:145]) if mid else ap("zero"),
+             ADD, ADD)
+    prev, cur = ap("cn", S_[0:3, 0:129:16]), ap("cn", S_[0:3, 16:145:16])
+    start, end = [(ap("up0"), prev), (ap("lo0"), cur)], [(ap("up1"), prev), (ap("lo1"), cur)]
+    if mid:
+        for k in range(3):
+            scan(ap("cn", S_[3 + k, 0:145]), ap("gl", S_[k, 0:145]), ap("zero"), ADD, ADD)
+        turn = start + [(ap("eye"), ap("cn", S_[3:6, 16:145:16])), (ap("eyen"), ap("cn", S_[3:6, 0:129:16]))]
     else:
-        if me == 3:
-            act(T.own[:], lto(3), "lt3", "own", 128, scale=-1.0, bias=1.0)
-        else:
-            tt(T.own[:], lto(hi), lto(lo), SUB, "lt%d lt%d" % (hi, lo), "own", 256)
-        tt(T.psz0[:, 0:128], T.epo[:], T.own[:], MUL, "epo own", "psz0", 256)
-    tt(T.dk[:], T.kk[:, 0:24], T.kk[:, 8:32], SUB, "kk0 kk1 kk2 kk3", "dk")
-    tt(T.acc[:, 0:128], T.kk[:, 24:32].indirect(T.bcl[:, 0:8]), T.npos[:], SUB, "kk3 bcl npos", "acc0", 220)
-    tt(T.acc[:, 128:512], T.dk[:].indirect(T.bcl[:, 0:24]), T.lto[:], MUL, "dk bcl lt1 lt2 lt3", "acc1", 620)
-    tt(T.psz0[:, 0:128], T.psz0[:, 0:128], T.acc[:, 0:128], ADD, "acc0", "psz0", 128)
-    tt(T.ac2[:, 0:128], T.acc[:, 128:256], T.acc[:, 256:384], ADD, "acc1", "ac2a", 256)
-    tt(T.psz0[:, 0:128], T.psz0[:, 0:128], T.acc[:, 384:512], ADD, "acc1", "psz0", 128)
-    tt(T.ac4[:], T.psz0[:, 0:128], T.ac2[:, 0:128], ADD, "ac2a psz0", "ac4", 128)
-    cp(T.fl[:], T.ac4[:].indirect(T.pml[:]), "ac4 pml", "fl", 220)
+        turn = end if me else start
+    mm([(ap("pst", S_[0:27]), end), (ap("pst", S_[27:54]), start), (ap("pst", S_[54:81]), turn)])
+    if me:
+        tt(off, ap("st"), ap("bb", S_[bnd[me]:bnd[me] + 4]), SUB)
+    tt(ap("xe"), by(ap("bb", S_[16:28]), bcl(4, 12)), ap("msk"), MUL)
+    mm([(ap("psw", S_[4 * k:4 * k + 4, 16 * h:16 * h + 16]), [(ap("bo32"), ap("xe", S_[64 * k:64 * k + 64]))])
+        for k in range(2) for h in range(2)])
 
-    zout = [T.psz0[:, 0:256], T.zs[:, 0:256], T.psz1[:, 0:256], T.zs[:, 256:512]]
-    for k, (f, key) in enumerate(zip((0, 32, 16, 48), ("psz0", "zs1", "psz1", "zs3"))):
-        c = slice(256 * k, 256 * k + 256)
-        act(T.gw[:, c], T.big[:].indirect(T.fl[:, 64 + f:80 + f]), "xs land fl", "gw%d" % k, 420, func=AF.Copy)
-        tt(T.df[:, c], T.big[:].indirect(T.fl[:, f:f + 16]), T.gw[:, c], SUB, "xs land fl gw%d" % k, "df%d" % k, 420)
-        act(zout[k], T.df[:, c], "df%d" % k, key, 256, func=AF.Abs)
-    tt(T.psz0[:, 0:256], T.psz0[:, 0:256], T.zs[:, 0:256], ADD, "zs1", "psz0", 256)
-    tt(T.tr[:, 0:256], T.psz1[:, 0:256], T.zs[:, 256:512], ADD, "psz1 zs3", "t1", 256)
-    tt(T.tr[:, 256:512], T.psz0[:, 0:256], T.tr[:, 0:256], ADD, "psz0 t1", "t2", 256)
-    tt(T.tr[:, 512:640], T.tr[:, 256:384], T.tr[:, 384:512], ADD, "t2", "t3", 256)
-    tt(T.ys[:].indirect(T.yl[:]), T.tr[:, 512:576], T.tr[:, 576:640], ADD, "t3 yl", "ys", 260)
-    load("s", T.y[:], T.ys[:], "sty", 16, "ys", "y", 2.0)
+    tt(ap("ci"), ap("pst", S_[0:81]), ap("zc"), ADD)
+    ts(ap("lm"), ap("ci", S_[27:81]), 15, AND)
+    cp(ap("lr", S_[:, 0:9]), ap("lm"))
+    ts(ap("dd"), ap("ci", S_[0:54]), 4, SHR)
+    tt(ap("last"), ap("dd", S_[0:27]), ap("dd", S_[27:54]), SUB)
+    tt(ap("hh"), ap("last"), ap("dd", S_[27:54]), MUL)
+    tt(ap("pl", S_[27:54]), ap("last"), ap("un1"), MUL)
+    tt(ap("pl", S_[0:27]), ap("hh"), ap("kc"), ADD)
+    cp(ap("ls", S_[:, 0:9]), ap("pl"))
+
+    def message(k):
+        c, m = S_[128 * k:128 * k + 128], S_[48 * k:48 * k + 48]
+        e0, q = EW * k, peers[k]
+        tt(ap("et", c), by(ap("wtab", S_[16 * k:16 * k + 16]), ap("lr", S_[3 + k, 0:8])), ap("crep", c), ADD)
+        ts(ap("eu", c), ap("et", c), 2, SHR, 1023, AND)
+        tt(ap("ep", c), ap("eu", c), ap("psw", S_[0:4]), MUL)
+        tt(ap("ee", S_[e0 + 1:e0 + 129]), ap("ep", c), ap("psw", S_[4:8]), ADD)
+        tt(ap("ea", S_[e0:e0 + 128]), by(ap("taba"), ap("lr", S_[k, 0:8])), ap("ee", S_[e0 + 1:e0 + 129]), ADD)
+        tt(ap("ea", S_[e0 + 1:e0 + 129]), by(ap("ee", S_[e0:e0 + 129]), ap("ls", S_[3 + k, 0:8])), ap("ea", S_[e0 + 1:e0 + 129]), MAX)
+        scan(ap("es", S_[k, 0:129]), ap("neg"), ap("ea", S_[e0:e0 + 129]), ADD, MAX)
+        cp(by(ap("win", S_[k]), ap("ls", S_[k, 0:9])), ap("es", S_[k]))
+        ts(ap("wm", m), ap("win", S_[k, 0:48]), R - 1, AND)
+        cp(ap("lst", m), ap("wm", m))
+        src = ap("outb", S_[CAP * k:CAP * k + CAP])
+        act(src, by(ap("big", S_[b0:b0 + R]), ap("lst", m)), AF.Copy, who=PLAN["out"][k])
+        rid, pid = topo.addr(T.cores[q], core)
+        at = _base(q, me)
+        rec("g", lambda: g.remote_dma(T.big[:, at:at + CAP], src[0], T.sem.darr, T.sem.dsent, pid, rid, _bits(dengs[k])),
+            [src] + ([key("sent0")] if k == 1 else []), [key("sent%d" % k)], 0.3, PLAN["sent"][k], ("", 0))
+
+    for k in range(3):
+        message(k)
+    rec("x", None, [key("sent%d" % k) for k in range(3)], [ap("big", S_[_base(me, q):_base(me, q) + CAP]) for q in peers],
+        0.0, 0.0, ("darr", darr))
+
+    fill(ap("big", S_[0:GAP]), 0)
+    for q in range(4):
+        e = _base(me, q) + (R if q == me else CAP)
+        fill(ap("big", S_[e:e + (OWNGAP if q == me else GAP)]), 0)
+    fill(ap("kk", S_[8 * me:8 * me + 8]), 0)
+    fill(ap("geo", S_[0:387:129]), 0)
+    fill(ap("rst"), 1)
+    fill(ap("rst", S_[0:387:129]), 0)
+    band(ap("lon"), ap("bon"), 1, A.is_gt)
+    band(ap("upn"), ap("bon"), -1, A.is_ge)
+    iota(ap("pm8"), [[1, 2], [16, 2], [8, 2]])
+    act(c1("col", 7), lane, scale=0.5)
+    act(c1("col", 8), l3, scale=31.5, bias=c1("col", 7))
+    act(c1("col", 9), lane, scale=4.0)
+    ts(ap("pml"), ap("pm8"), c1("col", 8), ADD)
+    ts(ap("yl"), xf(0, 4), c1("col", 9), ADD)
+    late = [ap("big", S_[b0:b0 + R])]
+    act(ap("u16"), ap("un", S_[0:8]), scale=16.0, after=late)
+    act(ap("ufo"), ap("ui", S_[384:512]), scale=1.0 / 1024, after=late)
+    mm([(ap("psa", S_[16 * k:16 * k + 16]), [(ap("bo16"), ap("sgn", S_[48:64]))]) for k in range(8)])
+    act(ap("rkw"), ap("psa", S_[0:128]), scale=-0.5, bias=7.5, after=late)
+    act(ap("nz"), ap("psz", S_[24:32]), after=late)
+    tt(ap("yp"), by(ap("nz"), bcl(0, 8)), ap("rkw"), ADD)
+    ts(ap("kap"), ap("yp"), 15, AND)
+    act(ap("offb"), off, bias=float(b0), after=late)
+    act(ap("nbb"), ap("bb", S_[0:20]), scale=-1.0, bias=2.0 ** -11, after=late)
+
+    def geo(b, a=0, n=128):
+        return ap("geo", S_[129 * b - 128 + a:129 * b - 128 + a + n])
+
+    en = "ps1" if me else "en"
+    for j in range(4):
+        c = S_[32 * j:32 * j + 32]
+        for b in (1, 2, 3):
+            act(geo(b, 32 * j, 32), ap("ufo", c), AF.Sign, c1("bb", 20 + j), c1("nbb", bnd[b] + j))
+        act(ap(en, c), ap("ufo", c), scale=c1("bb", 20 + j), bias=c1("offb", j))
+    scan(ap("co"), ap("rst"), ap("geo"), MUL, ADD)
+    groups = []
+    for q in peers:
+        terms = [(ap("eye"), ap("u16"))] if q in (0, 3) else []
+        for b, before, upto in ((q, "up1", "lo1"), (q + 1, "upn", "lon")):
+            if 0 < b < 4:
+                o = 129 * (b - 1)
+                terms += [(ap(before), ap("co", S_[o:o + 128:16])), (ap(upto), ap("co", S_[o + 16:o + 129:16]))]
+        groups.append((ap("psr", S_[8 * q:8 * q + 8]), terms))
+    mm(groups)
+    for q in peers:
+        c = S_[8 * q:8 * q + 8]
+        act(ap("kk", c), ap("psr", c), scale=0.5, bias=float(_base(me, q) - (8 if q else 0)))
+    yq = {q: ap("yq", S_[128 * q - 128:128 * q]) for q in peers if q}
+    for q in yq:
+        tt(yq[q], by(ap("kk"), bcl(8 * q, 8 * q + 8)), geo(q), MUL)
+    acc, (ya, yb) = ap("ps0", S_[0:128]), list(yq.values())[:2]
+    if me:
+        tt(ap("ye"), ap(en, S_[0:128]), geo(me), MUL)
+        tt(ya, by(ap("kk"), bcl(0, 8)), ya, MAX)
+        tt(acc, ya, yb, MAX)
+    else:
+        tt(acc, ya, yb, MAX)
+        tt(acc, acc, list(yq.values())[2], MAX)
+    tt(acc, acc, ap("kap"), ADD)
+    tt(ap("pos"), acc, ap("ye" if me else "en"), MAX)
+    cp(ap("fl"), by(ap("pos"), ap("pml")))
+
+    zout = [ap("ps0", S_[0:256]), ap("zs", S_[0:256]), ap("ps1", S_[0:256]), ap("zs", S_[256:512])]
+    for k, f in enumerate((0, 32, 16, 48)):
+        c = S_[256 * k:256 * k + 256]
+        act(ap("gw", c), by(ap("big"), ap("fl", S_[64 + f:80 + f])), AF.Copy, who="a")
+        tt(ap("df", c), by(ap("big"), ap("fl", S_[f:f + 16])), ap("gw", c), SUB)
+        act(zout[k], ap("df", c), AF.Abs)
+    tt(zout[0], zout[0], zout[1], ADD)
+    tt(ap("tr", S_[0:256]), zout[2], zout[3], ADD)
+    tt(ap("ps1", S_[256:384]), ap("ps0", S_[0:128]), ap("tr", S_[0:128]), ADD)
+    tt(ap("tr", S_[256:384]), ap("ps0", S_[128:256]), ap("tr", S_[128:256]), ADD)
+    tt(ap("tr", S_[384:512]), ap("ps1", S_[256:384]), ap("tr", S_[256:384]), ADD)
+    tt(by(ap("ys"), ap("yl")), ap("tr", S_[384:448]), ap("tr", S_[448:512]), ADD)
+    load("s", T.y[:], T.ys[:], "sty", 16, [ap("ys")], [], PLAN["small"])
 
     queue = {"v": V, "a": S, "t": PE, "g": g, "s": SY}
     semof = {"v": "sv", "a": "sa", "t": "st", "g": "sg"}
     count = {"v": 0, "a": 0, "t": 0, "g": 0}
     waited, bank = {}, {}
-    order = _arrange(ops)
-    for o in order:
+    for o in _arrange(ops):
         q = o["q"]
         if q == "x":
             continue
         evs = [ops[d]["ev"] for d in o["d"]]
-        banks = [k for k in o["r"] + o["w"] if k.startswith("ps")]
-        evs += [ev for k in banks for ev in bank.get(k, []) if ev[0] != semof[q]]
+        evs += [ev for k in o["banks"] for ev in bank.get(k, []) if ev[0] != semof[q]]
         deps = {}
         for ev in evs:
             if ev is not None and ev[1]:
                 deps[ev[0]] = max(deps.get(ev[0], 0), ev[1])
-        for sname, val in deps.items():
-            if waited.get((q, sname), 0) < val and not (q == "g" and sname == "go"):
-                queue[q].wait_ge(T.sem[sname], val)
-                waited[(q, sname)] = val
+        for sname, v in deps.items():
+            if waited.get((q, sname), 0) < v:
+                queue[q].wait_ge(T.sem[sname], v)
+                waited[(q, sname)] = v
         if o["ev"] is None:
             count[q] += 1
             o["make"]().then_inc(T.sem[semof[q]], 1)
             o["ev"] = (semof[q], count[q])
         else:
             o["make"]()
-        for k in banks:
+        for k in o["banks"]:
             bank.setdefault(k, []).append(o["ev"])
 
     g.wait_ge(T.sem.csent, sum(len(e) for e in cengs))

import numpy as np
from concourse.bass import DstId, RemoteDMATransfer
from concourse.mybir import AluOpType, ActivationFunctionType

F32, I32, U16, BF, F16 = "float32", "int32", "uint16", "bfloat16", "float16"
R, CAP = 4096, 768
GAP, OWNGAP = 32, 544
BIG = GAP + 3 * (CAP + GAP) + R + OWNGAP
STEP, LOW = 8192.0, -float(2 ** 21)
WIN, EW = 208, 136
SPLIT = 4096
ACTINT = True

_SB = {
    BF: dict(xin=R, big=BIG, outb=3 * CAP, bo16=128, bon=128, eye=128, eyen=128, eye15=128, lo0=128, lo1=128, up0=128, up1=128,
             lon=128, upn=128, zm=144, sgn=64, gl=(6, 146), zero=145, geo=387, rst=387, u16=8, gw=1024, neg=129),
    I32: dict(idxi=256, cl=20, abz=8, pci=4, tb=512, ui=512, kwi=128, kwa=128, ci=81, lm=54, dd=54, et=384, eu=384, ee=3 * EW,
              win=(3, WIN), wm=144, yp=128, kap=128, pos=128),
    U16: dict(idxu=256, ucl=40, pml=8, yl=4, lr=(6, 10), ls=(6, 10), lst=144, fl=128),
    F16: dict(uf=(4, 128), cn=(6, 146), co=387, inc=6, hr=(3, 32)),
    F32: dict(abf=8, abv=8, a16=4, col=12, xk=152, dist=128, bo32=128, bos=128, i128=128, kwf=128, rk2=4, wc=4, i2=32, nb=128,
              n0r=128, crep=384, wtab=48, msk=128, tab0=16, taba=16, uc0=27, kc=27, un=27, un1=27, zc=(9, 9), cf=5, st=4, bb=28,
              xe=128, last=27, hh=27, pl=54, ep=384, ea=3 * EW, es=(3, 144), pm8=8, rkw=128, nz=8, kk=32, offb=4, nbb=20,
              ufo=128, en=128, ye=128, yq=384, df=1024, zs=512, tr=512, ys=64),
}
SHAPE = {n: (list(s) if isinstance(s, tuple) else [s]) for t in _SB.values() for n, s in t.items()}
SCRATCH = {n: ("sbuf", [128] + SHAPE[n], d) for d, t in _SB.items() for n in t}
PSUM = ("psa", "psz", "psh", "psw", "pst", "psr", "ps0", "ps1")
SHAPE.update({n: [16, 32] if n == "psw" else [512] for n in PSUM})
SCRATCH.update({n: ("psum", [128] + SHAPE[n], F32) for n in PSUM})
SEMAPHORES = ["sv", "sa", "st", "sg", "ldc", "lda", "ldi", "ldx", "carr", "csent", "darr", "dsent", "sty"]

A = AluOpType
AF = ActivationFunctionType
S_ = np.s_
PLAN = dict(small=1.5, rows=3.9, counts=2.6, sent=(2.0, 3.0, 2.5), wake=0.08, call=0.04, cycle=0.00095, gather=1.55, scatter=3.7,
            slack=0.04, pieces=[(0, R, "a")], out="aav", halves=((0, 2), (2, 4)),
            first=dict(n0r=3, uc0=3, i2=2, idxu=1, kwi=1, kwa=1, psh=1, outb=1),
            scalar="abf abv a16 kwf wc uf ufo crep cf un un1 kc zc taba msk".split(), vector=["wtab"],
            early="crep wc uf taba msk un1 kc cf".split())


def _bits(engs):
    m = 0
    for e in engs:
        m |= 1 << e
    return m


def _peers(rank, T, topo):
    c = T.cores[rank]
    others = [q for q in range(len(T.cores)) if q != rank]
    near = [q for q in others if T.cores[q] in topo.cores_of(c)]
    far = [q for q in others if q not in near]
    return (far if rank > near[0] else far[::-1]) + near


def _count_engines(rank, T, topo):
    c = T.cores[rank]
    used, out = [], []
    for q in _peers(rank, T, topo):
        e = [k for k in topo.engines(c, T.cores[q]) if k not in used][:4]
        used += e
        out.append(e)
    return out


def _data_engines(rank, T, topo):
    c = T.cores[rank]
    peers = _peers(rank, T, topo)
    far = set()
    for q in peers:
        if T.cores[q] not in topo.cores_of(c):
            far |= set(topo.engines(c, T.cores[q]))
    out = []
    for q in peers:
        e = topo.engines(c, T.cores[q])
        if T.cores[q] in topo.cores_of(c):
            e = [k for k in e if k not in far] or e
        out.append(e)
    return out


def _base(rank, q):
    return GAP + sum(R + OWNGAP if t == rank else CAP + GAP for t in range(q))


def _arrange(ops):
    level = [0.0] * len(ops)
    for n in range(len(ops) - 1, -1, -1):
        level[n] += ops[n]["c"] + ops[n]["lat"] + PLAN["first"].get(ops[n]["name"], 0.0)
        for d in ops[n]["d"]:
            level[d] = max(level[d], level[n])
    end, free, out, left = {}, {}, [], list(range(len(ops)))
    while left:
        can = []
        for n in left:
            if all(d in end for d in ops[n]["d"]):
                ready = max([0.0] + [end[d] for d in ops[n]["d"]])
                can += [(max(free.get(q, 0.0), ready), q, n) for q in ops[n]["on"]]
        t0, q0, n0 = min(can)
        _, n, t = max((level[m], -m, t) for t, q, m in can if q == q0 and t <= t0 + PLAN["slack"])
        n = -n
        ops[n]["q"], ops[n]["make"] = q0, ops[n]["on"][q0]
        if ops[n]["q"] != "x":
            free[ops[n]["q"]] = t + ops[n]["c"]
        end[n] = t + ops[n]["c"] + ops[n]["lat"]
        left.remove(n)
        out.append(ops[n])
    return out


def rank_program(g, core, T, topo):
    me = T.rank_of(core)
    if me is None:
        return
    peers = _peers(me, T, topo)
    slots = peers + [me]
    mid = 1 if 0 < me < 3 else 0
    V, S, PE, SY = g.vector, g.scalar, g.tensor, g.sync
    ops, touched = [], {}
    CY = PLAN["cycle"]

    def ap(name, ix=S_[:]):
        ix = ix if isinstance(ix, tuple) else (ix,)
        cols = np.zeros(SHAPE[name], bool)
        cols[ix] = True
        return T[name][(S_[:],) + ix], [(name, int.from_bytes(bytes(np.packbits(cols)), "big"))], int(cols.sum()), False

    def c1(name, j):
        return ap(name, S_[j:j + 1])

    def by(win, off):
        return win[0].indirect(off[0]), win[1] + off[1], 16 * off[2], True

    def key(name):
        return None, [(name, 1)], 0, False

    def rec(q, make, r, w, c, lat=PLAN["wake"], ev=None):
        n, d = len(ops), set()
        r = [t for x in r if isinstance(x, tuple) for t in x[1]]
        w = [t for x in w for t in x[1][:1]], [t for x in w for t in x[1][1:]]
        for wr, items in ((False, r + w[1]), (True, w[0])):
            for name, m in items:
                d |= {k for k, km, kw in touched.get(name, []) if k != n and km & m and (wr or kw)}
                touched.setdefault(name, []).append((n, m, wr))
        ops.append(dict(on=make if q == "va" else {q: make}, d=d, c=c, name=w[0][0][0] if w[0] else "", lat=lat, ev=ev, banks={nm for nm, m in r + w[0] if nm in PSUM}))

    def val(x):
        return x[0] if isinstance(x, tuple) else x

    def cost(o, ins, per=1.0):
        if o[3] or ins[0][3]:
            return 0.06 + CY * PLAN["scatter" if o[3] else "gather"] * o[2]
        return PLAN["call"] + CY * max(64, per * o[2])

    def half(*xs):
        return 0.5 if all(SCRATCH[x[1][0][0]][2] in (BF, F16, U16) for x in xs) else 1.0

    def mm(items, after=(), first=True, last=True):
        def make():
            for o, terms in items:
                for k, (l, rh) in enumerate(terms):
                    ins = PE.matmul(o[0], l[0], rh[0], first and k == 0, last and k == len(terms) - 1)
            return ins
        c = sum(max(64, rh[2]) * (4 if SCRATCH[l[1][0][0]][2] == F32 else 1) for o, terms in items for l, rh in terms)
        rec("t", make, [x for o, terms in items for t in terms for x in t] + list(after), [o for o, t in items], CY * c)

    def ts(o, a, s1, op0, s2=None, op1=None, after=()):
        more = () if op1 is None else (op1,)
        rec("v", lambda: V.tensor_scalar(o[0], a[0], val(s1), val(s2), op0, *more), [a, s1, s2] + list(after), [o],
            cost(o, [a], half(o, a)))

    def tt(o, a, b, op):
        both = a[1][0][0] not in PSUM and b[1][0][0] not in PSUM
        rec("v", lambda: V.tensor_tensor(o[0], a[0], b[0], op), [a, b], [o], cost(o, [a], 2.0 if both else 1.0))

    def cp(o, a, after=()):
        rec("v", lambda: V.tensor_copy(o[0], a[0]), [a] + list(after), [o], cost(o, [a], half(o, a)))

    def scan(o, d0, d1, o0, o1):
        rec("v", lambda: V.tensor_tensor_scan(o[0], d0[0], d1[0], 0.0, o0, o1), [d0, d1], [o], cost(o, [d0], half(o, d0, d1)))

    def act(o, a, func=AF.Identity, scale=1.0, bias=0.0, accum=None, after=(), who="va"):
        kw = {} if func == AF.Copy else dict(scale=val(scale), bias=val(bias))
        if accum:
            kw["accum_out"] = accum[0]
        on = dict(a=lambda: S.activation(o[0], a[0], func, **kw))
        if func == AF.Copy:
            on["v"] = lambda: V.tensor_copy(o[0], a[0])
        if func == AF.Identity:
            on["v"] = lambda: V.tensor_scalar(o[0], a[0], val(scale), val(bias), A.mult, A.add)
        who = "a" if o[1][0][0] in PLAN["scalar"] else "v" if o[1][0][0] in PLAN["vector"] else who
        rec("va", {q: on[q] for q in who if q in on}, [a, scale, bias] + list(after), [o] + ([accum] if accum else []), cost(o, [a]))

    def iota(o, pattern, base=0, cm=0, late=True):
        kw = {} if SCRATCH[o[1][0][0]][2] == I32 else dict(allow_small_or_imprecise_dtypes=True)
        rec("g", lambda: g.iota(o[0], pattern, base, cm, **kw), [key("go")] if late else [], [o], 0.13 + 2 * CY * o[2])

    def fill(o, v, who="g"):
        if who == "g":
            iota(o, [[0, o[2]]], int(v))
        else:
            rec("v", lambda: V.memset(o[0], v), [], [o], cost(o, [o], half(o)))

    def band(o, src, step, cmp):
        rec("g", lambda: g.affine_select(o[0], src[0], [[step, 128]], cmp, 0.0, 0, -step), [key("go"), src], [o], 0.42)

    def load(q, out, in_, sem, v, r, w, lat):
        rec(q, lambda: (SY if q == "s" else S).dma_start(out, in_).then_inc(T.sem[sem], 16), r, w, 0.05, lat, (sem, v))

    SHR, AND, MUL, ADD, SUB, MAX = A.arith_shift_right, A.bitwise_and, A.mult, A.add, A.subtract, A.max
    cengs, dengs = _count_engines(me, T, topo), _data_engines(me, T, topo)
    carr = sum(len(_count_engines(q, T, topo)[_peers(q, T, topo).index(me)]) for q in peers)
    darr = sum(len(_data_engines(q, T, topo)[_peers(q, T, topo).index(me)]) for q in peers)
    mine = ap("cl", S_[4 + 4 * me:8 + 4 * me])
    b0 = _base(me, me)
    tofloat = act if ACTINT else cp

    load("s", mine[0], T.counts[:], "ldc", 16, [], [mine], PLAN["small"])
    rec("v", lambda: V.memset(T.abz[:], 0), [], [ap("abz")], 0.1)
    load("s", T.abz[0:128:16, :], T.ab[:], "lda", 16, [], [ap("abz")], PLAN["small"])
    load("a", T.idxi[:], T.idx[:], "ldi", 16, [], [ap("idxi")], PLAN["small"] + 0.2)
    rec("x", None, [], [key("behind")], 0.0, 0.3)
    load("s", T.xin[:], T.x[:], "ldx", 16, [key("behind")], [ap("xin")], PLAN["rows"])

    def send_counts():
        trs = []
        for q, e in zip(peers, cengs):
            rid, pid = topo.addr(T.cores[q], core)
            trs.append(RemoteDMATransfer(dst_ids=[DstId(rid=rid, pnc=pid)], dma_engine_mask=_bits(e), remote_sem=T.sem.carr,
                                         src=mine[0], dst=mine[0]))
        g.remote_dma_fused(trs, local_sem=T.sem.csent)

    rec("g", send_counts, [mine], [key("go")], 0.3, 0.0, ("", 0))
    rec("x", None, [key("go")], [ap("cl", S_[4 + 4 * q:8 + 4 * q]) for q in peers], 0.0, PLAN["counts"], ("carr", carr))

    def xf(a, b):
        return ap("xk", S_[8 + a:8 + b])

    def bcl(a, b):
        return ap("ucl", S_[8 + a:8 + b])

    iota(c1("pci", 0), [[0, 1]], 0, 1, False)
    iota(xf(0, 144), [[1, 144]], 0, 0, False)
    iota(ap("i128", S_[0:64]), [[0, 4], [1, 16]], 0, 0, False)
    iota(ap("xk", S_[0:8]), [[0, 2], [slots[2] - slots[0], 2], [slots[1] - slots[0], 2]], slots[0], 0, False)
    for k, m in enumerate((15, 112, 3)):
        ts(c1("pci", k + 1), c1("pci", 0), m, AND)
    cp(ap("col", S_[0:4]), ap("pci"))
    part, lane, g16, l3 = c1("col", 0), c1("col", 1), c1("col", 2), c1("col", 3)
    act(c1("col", 4), g16, scale=-1.0, bias=-7.5)
    act(ap("dist"), xf(0, 128), AF.Abs, bias=c1("col", 4))
    ts(ap("bo32"), ap("dist"), 8.0, A.is_lt)
    act(ap("bo16"), ap("bo32"))
    act(ap("bon"), ap("bo32"), scale=-1.0)
    act(ap("bos"), ap("bo32"), scale=1.0 / 65536)
    ts(ap("eye"), xf(0, 128), part, A.is_equal)
    act(ap("eyen"), ap("eye"), scale=-1.0)
    act(ap("eye15"), ap("eye"), scale=15.0)
    act(c1("col", 5), lane, scale=128.0)
    act(ap("nb"), xf(0, 128), bias=c1("col", 5))
    act(ap("i128", S_[64:128]), xf(0, 64), scale=0.0, bias=lane)
    cp(ap("ucl"), ap("xk", S_[0:40]))
    act(c1("col", 6), g16, bias=15.0)
    ts(ap("zm"), xf(0, 144), c1("col", 6), A.is_equal)
    act(c1("col", 10), lane, scale=-1.0 / 16, bias=-2048.0)
    iota(ap("i2"), [[0, 2], [-2, 16]], 15)
    iota(ap("n0r"), [[16, 8], [128, 16]])
    band(ap("lo0"), ap("bo16"), 1, A.is_gt)
    band(ap("up0"), ap("bo16"), -1, A.is_ge)
    band(ap("lo1"), ap("bo16"), 1, A.is_ge)
    band(ap("up1"), ap("bo16"), -1, A.is_gt)
    iota(ap("uc0"), [[0, 3], [16, 9]])
    act(ap("un"), ap("uc0"), bias=lane)
    act(ap("kc"), ap("un"), bias=64.0)
    act(ap("zc", S_[3:6]), ap("un"), scale=-16.0 * (1 + mid), bias=-1024.0)
    act(ap("zc", S_[0:3]), ap("un"), scale=-16.0 * (1 + mid), bias=-1024.0 - 16 * mid)
    act(ap("un1"), ap("un"), bias=1.0)
    fill(ap("zc", S_[6:9, 8:9]), 0)
    ts(ap("msk", S_[0:64]), ap("i128", S_[0:64]), lane, A.is_equal, 1.0 / 1024, MUL)
    act(ap("msk", S_[64:128]), ap("msk", S_[0:64]), scale=1024.0)
    ts(ap("tab0"), xf(0, 16), lane, A.is_le)
    act(ap("taba"), ap("tab0"), scale=STEP - LOW, bias=LOW)
    fill(ap("cl", S_[0:4]), 0)
    fill(c1("cf", 0), 0, "v")
    fill(ap("zero"), 0, "v")
    fill(ap("neg"), -STEP)
    fill(ap("gl", S_[:, 0:1]), 0)
    fill(ap("gl", S_[:, 129:145]), 1)
    fill(ap("ee", S_[0:3 * EW:EW]), LOW)
    fill(ap("ea", S_[128:3 * EW:EW]), LOW)
    fill(ap("es", S_[:, 129:144]), 0)
    fill(ap("win", S_[:, 0:48]), 0)

    tofloat(ap("abf"), ap("abz"))
    mm([(ap("psa", S_[0:8]), [(ap("bo32"), ap("abf"))])])
    act(ap("abv"), ap("psa", S_[0:8]))
    ac = [c1("abv", 2 * q) for q in slots]
    bc = [c1("abv", 2 * q + 1) for q in slots]
    for k in range(4):
        ts(ap("tb", S_[128 * k:128 * k + 128]), ap("nb"), ac[k], MUL, bc[k], ADD)
    for a, b in PLAN["halves"]:
        ts(ap("ui", S_[128 * a:128 * b]), ap("tb", S_[128 * a:128 * b]), 2, SHR, 1023, AND)
        act(ap("uf", S_[a:b]), ap("ui", S_[128 * a:128 * b]), scale=1.0 / 1024)
    for k in range(3):
        act(ap("crep", S_[128 * k:128 * k + 128]), ap("n0r"), scale=ac[k], bias=bc[k])
    act(ap("a16"), ap("psa", S_[0:8:2]), scale=16.0, bias=1.0)
    tt(ap("kwi"), by(ap("a16"), ap("ucl", S_[0:8])), ap("i128"), MUL)
    ts(ap("kwa"), ap("kwi"), 65535, AND)
    tofloat(ap("kwf"), ap("kwa"))
    act(ap("wc"), ap("kwf", S_[64:128:16]), scale=1.0 / 16, bias=c1("col", 10))
    for k in range(4):
        c = S_[16 * k:16 * k + 16]
        act(ap("sgn", c), ap("kwf", c), AF.Sign, -1.0, c1("kwf", 64 + 16 * k), c1("rk2", k))
    for k in range(3):
        ts(ap("hr", S_[k]), ap("i2"), c1("rk2", k), A.is_equal, c1("wc", k), MUL)
    mm([(ap("psh", S_[0:48]), [(ap("zm", S_[15 - k:143 - k]), ap("hr", S_[:, 15 - k:31 - k])) for k in range(16)])])
    act(ap("wtab"), ap("psh", S_[0:48]), bias=2048.0)
    mm([(ap("psz", S_[0:32]), [(ap("bos"), ap("kwf", S_[64:128:2]))])], last=False)
    mm([(ap("psz", S_[0:32]), [(ap("eyen" if i else "eye15"), ap("uf", S_[:, i:128:16])) for i in range(16)])], first=False)
    cp(ap("zc", S_[6:9, 0:8]), ap("psz", S_[0:24]))
    tofloat(ap("cf", S_[1:5]), mine)
    scan(ap("inc", S_[0:5]), ap("cf"), ap("zero", S_[0:5]), ADD, ADD)
    mm([(c1("psr", 64), [(ap("lo0"), c1("inc", 4))])])
    off = ap("bb", S_[24:28])
    ts(ap("st") if me else off, ap("inc", S_[0:4]), c1("psr", 64), ADD, -0.5 + 2.0 ** -11, ADD)

    cp(ap("idxu"), ap("idxi"))
    for a, b, who in PLAN["pieces"]:
        act(ap("big", S_[b0 + a:b0 + b]), by(ap("xin"), ap("idxu", S_[a // 16:b // 16])), AF.Copy, who=who,
            after=[ap(n) for n in PLAN["early"]] + [ap("rk2", S_[0:3]), ap("zc", S_[0:6])])

    tt(ap("bb", S_[0:16]), ap("cl", S_[0:16]), ap("cl", S_[4:20]), ADD)
    tt(ap("bb", S_[16:24]), ap("bb", S_[0:8]), ap("bb", S_[8:16]), ADD)
    bnd = {1: 0, 2: 4, 3: 16}
    for j in range(4):
        c = S_[32 * j + 1:32 * j + 33]
        u = ap("uf", S_[0:3, 32 * j:32 * j + 32])
        if me != 0:
            ts(ap("gl", S_[0:3, c]), u, c1("bb", 20 + j), MUL, c1("bb", bnd[me] + j), A.is_ge)
        if me != 3:
            ts(ap("gl", S_[3:6, c]), u, c1("bb", 20 + j), MUL, c1("bb", bnd[me + 1] + j), A.is_lt)
    for k in range(3):
        scan(ap("cn", S_[k, 0:145]), ap("gl", S_[k if me else 3 + k, 0:145]), ap("gl", S_[3 + k, 0:145]) if mid else ap("zero"),
             ADD, ADD)
    prev, cur = ap("cn", S_[0:3, 0:129:16]), ap("cn", S_[0:3, 16:145:16])
    start, end = [(ap("up0"), prev), (ap("lo0"), cur)], [(ap("up1"), prev), (ap("lo1"), cur)]
    if mid:
        for k in range(3):
            scan(ap("cn", S_[3 + k, 0:145]), ap("gl", S_[k, 0:145]), ap("zero"), ADD, ADD)
        turn = start + [(ap("eye"), ap("cn", S_[3:6, 16:145:16])), (ap("eyen"), ap("cn", S_[3:6, 0:129:16]))]
    else:
        turn = end if me else start
    mm([(ap("pst", S_[0:27]), end), (ap("pst", S_[27:54]), start), (ap("pst", S_[54:81]), turn)])
    if me:
        tt(off, ap("st"), ap("bb", S_[bnd[me]:bnd[me] + 4]), SUB)
    tt(ap("xe"), by(ap("bb", S_[16:28]), bcl(4, 12)), ap("msk"), MUL)
    mm([(ap("psw", S_[4 * k:4 * k + 4, 16 * h:16 * h + 16]), [(ap("bo32"), ap("xe", S_[64 * k:64 * k + 64]))])
        for k in range(2) for h in range(2)])

    tt(ap("ci"), ap("pst", S_[0:81]), ap("zc"), ADD)
    ts(ap("lm"), ap("ci", S_[27:81]), 15, AND)
    cp(ap("lr", S_[:, 0:9]), ap("lm"))
    ts(ap("dd"), ap("ci", S_[0:54]), 4, SHR)
    tt(ap("last"), ap("dd", S_[0:27]), ap("dd", S_[27:54]), SUB)
    tt(ap("hh"), ap("last"), ap("dd", S_[27:54]), MUL)
    tt(ap("pl", S_[27:54]), ap("last"), ap("un1"), MUL)
    tt(ap("pl", S_[0:27]), ap("hh"), ap("kc"), ADD)
    cp(ap("ls", S_[:, 0:9]), ap("pl"))

    def message(k):
        c, m = S_[128 * k:128 * k + 128], S_[48 * k:48 * k + 48]
        e0, q = EW * k, peers[k]
        tt(ap("et", c), by(ap("wtab", S_[16 * k:16 * k + 16]), ap("lr", S_[3 + k, 0:8])), ap("crep", c), ADD)
        ts(ap("eu", c), ap("et", c), 2, SHR, 1023, AND)
        tt(ap("ep", c), ap("eu", c), ap("psw", S_[0:4]), MUL)
        tt(ap("ee", S_[e0 + 1:e0 + 129]), ap("ep", c), ap("psw", S_[4:8]), ADD)
        tt(ap("ea", S_[e0:e0 + 128]), by(ap("taba"), ap("lr", S_[k, 0:8])), ap("ee", S_[e0 + 1:e0 + 129]), ADD)
        tt(ap("ea", S_[e0 + 1:e0 + 129]), by(ap("ee", S_[e0:e0 + 129]), ap("ls", S_[3 + k, 0:8])), ap("ea", S_[e0 + 1:e0 + 129]), MAX)
        scan(ap("es", S_[k, 0:129]), ap("neg"), ap("ea", S_[e0:e0 + 129]), ADD, MAX)
        cp(by(ap("win", S_[k]), ap("ls", S_[k, 0:9])), ap("es", S_[k]))
        ts(ap("wm", m), ap("win", S_[k, 0:48]), R - 1, AND)
        cp(ap("lst", m), ap("wm", m))
        src = ap("outb", S_[CAP * k:CAP * k + CAP])
        act(src, by(ap("big", S_[b0:b0 + R]), ap("lst", m)), AF.Copy, who=PLAN["out"][k])
        rid, pid = topo.addr(T.cores[q], core)
        at = _base(q, me)
        rec("g", lambda: g.remote_dma(T.big[:, at:at + CAP], src[0], T.sem.darr, T.sem.dsent, pid, rid, _bits(dengs[k])),
            [src] + ([key("sent0")] if k == 1 else []), [key("sent%d" % k)], 0.3, PLAN["sent"][k], ("", 0))

    for k in range(3):
        message(k)
    rec("x", None, [key("sent%d" % k) for k in range(3)], [ap("big", S_[_base(me, q):_base(me, q) + CAP]) for q in peers],
        0.0, 0.0, ("darr", darr))

    fill(ap("big", S_[0:GAP]), 0)
    for q in range(4):
        e = _base(me, q) + (R if q == me else CAP)
        fill(ap("big", S_[e:e + (OWNGAP if q == me else GAP)]), 0)
    fill(ap("kk", S_[8 * me:8 * me + 8]), 0)
    fill(ap("geo", S_[0:387:129]), 0)
    fill(ap("rst"), 1)
    fill(ap("rst", S_[0:387:129]), 0)
    band(ap("lon"), ap("bon"), 1, A.is_gt)
    band(ap("upn"), ap("bon"), -1, A.is_ge)
    iota(ap("pm8"), [[1, 2], [16, 2], [8, 2]])
    act(c1("col", 7), lane, scale=0.5)
    act(c1("col", 8), l3, scale=31.5, bias=c1("col", 7))
    act(c1("col", 9), lane, scale=4.0)
    ts(ap("pml"), ap("pm8"), c1("col", 8), ADD)
    ts(ap("yl"), xf(0, 4), c1("col", 9), ADD)
    late = [ap("big", S_[b0:b0 + R])]
    act(ap("u16"), ap("un", S_[0:8]), scale=16.0, after=late)
    act(ap("ufo"), ap("ui", S_[384:512]), scale=1.0 / 1024, after=late)
    mm([(ap("psa", S_[16 * k:16 * k + 16]), [(ap("bo16"), ap("sgn", S_[48:64]))]) for k in range(8)])
    act(ap("rkw"), ap("psa", S_[0:128]), scale=-0.5, bias=7.5, after=late)
    act(ap("nz"), ap("psz", S_[24:32]), after=late)
    tt(ap("yp"), by(ap("nz"), bcl(0, 8)), ap("rkw"), ADD)
    ts(ap("kap"), ap("yp"), 15, AND)
    act(ap("offb"), off, bias=float(b0), after=late)
    act(ap("nbb"), ap("bb", S_[0:20]), scale=-1.0, bias=2.0 ** -11, after=late)

    def geo(b, a=0, n=128):
        return ap("geo", S_[129 * b - 128 + a:129 * b - 128 + a + n])

    en = "ps1" if me else "en"
    for j in range(4):
        c = S_[32 * j:32 * j + 32]
        for b in (1, 2, 3):
            act(geo(b, 32 * j, 32), ap("ufo", c), AF.Sign, c1("bb", 20 + j), c1("nbb", bnd[b] + j))
        act(ap(en, c), ap("ufo", c), scale=c1("bb", 20 + j), bias=c1("offb", j))
    scan(ap("co"), ap("rst"), ap("geo"), MUL, ADD)
    groups = []
    for q in peers:
        terms = [(ap("eye"), ap("u16"))] if q in (0, 3) else []
        for b, before, upto in ((q, "up1", "lo1"), (q + 1, "upn", "lon")):
            if 0 < b < 4:
                o = 129 * (b - 1)
                terms += [(ap(before), ap("co", S_[o:o + 128:16])), (ap(upto), ap("co", S_[o + 16:o + 129:16]))]
        groups.append((ap("psr", S_[8 * q:8 * q + 8]), terms))
    mm(groups)
    for q in peers:
        c = S_[8 * q:8 * q + 8]
        act(ap("kk", c), ap("psr", c), scale=0.5, bias=float(_base(me, q) - (8 if q else 0)))
    yq = {q: ap("yq", S_[128 * q - 128:128 * q]) for q in peers if q}
    for q in yq:
        tt(yq[q], by(ap("kk"), bcl(8 * q, 8 * q + 8)), geo(q), MUL)
    acc, (ya, yb) = ap("ps0", S_[0:128]), list(yq.values())[:2]
    if me:
        tt(ap("ye"), ap(en, S_[0:128]), geo(me), MUL)
        tt(ya, by(ap("kk"), bcl(0, 8)), ya, MAX)
        tt(acc, ya, yb, MAX)
    else:
        tt(acc, ya, yb, MAX)
        tt(acc, acc, list(yq.values())[2], MAX)
    tt(acc, acc, ap("kap"), ADD)
    tt(ap("pos"), acc, ap("ye" if me else "en"), MAX)
    cp(ap("fl"), by(ap("pos"), ap("pml")))

    zout = [ap("ps0", S_[0:256]), ap("zs", S_[0:256]), ap("ps1", S_[0:256]), ap("zs", S_[256:512])]
    for k, f in enumerate((0, 32, 16, 48)):
        c = S_[256 * k:256 * k + 256]
        act(ap("gw", c), by(ap("big"), ap("fl", S_[64 + f:80 + f])), AF.Copy, who="a")
        tt(ap("df", c), by(ap("big"), ap("fl", S_[f:f + 16])), ap("gw", c), SUB)
        act(zout[k], ap("df", c), AF.Abs)
    tt(zout[0], zout[0], zout[1], ADD)
    tt(ap("tr", S_[0:256]), zout[2], zout[3], ADD)
    tt(ap("ps1", S_[256:384]), ap("ps0", S_[0:128]), ap("tr", S_[0:128]), ADD)
    tt(ap("tr", S_[256:384]), ap("ps0", S_[128:256]), ap("tr", S_[128:256]), ADD)
    tt(ap("tr", S_[384:512]), ap("ps1", S_[256:384]), ap("tr", S_[256:384]), ADD)
    tt(by(ap("ys"), ap("yl")), ap("tr", S_[384:448]), ap("tr", S_[448:512]), ADD)
    load("s", T.y[:], T.ys[:], "sty", 16, [ap("ys")], [], PLAN["small"])

    queue = {"v": V, "a": S, "t": PE, "g": g, "s": SY}
    semof = {"v": "sv", "a": "sa", "t": "st", "g": "sg"}
    count = {"v": 0, "a": 0, "t": 0, "g": 0}
    waited, bank = {}, {}
    for o in _arrange(ops):
        q = o["q"]
        if q == "x":
            continue
        evs = [ops[d]["ev"] for d in o["d"]]
        evs += [ev for k in o["banks"] for ev in bank.get(k, []) if ev[0] != semof[q]]
        deps = {}
        for ev in evs:
            if ev is not None and ev[1]:
                deps[ev[0]] = max(deps.get(ev[0], 0), ev[1])
        for sname, v in deps.items():
            if waited.get((q, sname), 0) < v:
                queue[q].wait_ge(T.sem[sname], v)
                waited[(q, sname)] = v
        if o["ev"] is None:
            count[q] += 1
            o["make"]().then_inc(T.sem[semof[q]], 1)
            o["ev"] = (semof[q], count[q])
        else:
            o["make"]()
        for k in o["banks"]:
            bank.setdefault(k, []).append(o["ev"])

    g.wait_ge(T.sem.csent, sum(len(e) for e in cengs))
    g.wait_ge(T.sem.dsent, sum(len(e) for e in dengs))
    for q in ("g", "a", "t", "v"):
        g.wait_ge(T.sem[semof[q]], count[q])
    g.wait_ge(T.sem.sty, 16)
